import numpy as np, ml_dtypes
CORES = [36,164,52,180,100,228,116,244]
N = 8
import mx_ref
BF = ml_dtypes.bfloat16
def gentries(a):
    return np.ascontiguousarray(a.reshape(8, 16, -1).transpose(0, 2, 1)).reshape(8, -1)
def gtable(e):
    e = np.asarray(e); return np.ascontiguousarray(e.reshape(8, -1, 16).transpose(0, 2, 1)).reshape(128, -1).astype(np.int32)
def gcols(t, e):
    v = np.concatenate([t.reshape(8, 16, -1, 4), np.zeros((8, 16, 1, 4), BF)], axis=2)
    return np.ascontiguousarray(np.stack([v[g][:, e[g]] for g in range(8)])).reshape(128, -1)
def tile(rs):
    return np.stack(rs, axis=2).reshape(128, -1).astype(BF)
def pick(q, e):
    c = np.concatenate([q[0].reshape(128, -1, 4), np.zeros((128, 1, 4), np.uint8)], axis=1); s = np.concatenate([q[1], np.ones((16, 1), np.uint8)], axis=1)
    return (np.ascontiguousarray(c[:, e].reshape(128, -1)), np.ascontiguousarray(s[:, e]))
def join(*qs):
    return (np.concatenate([q[0] for q in qs], axis=1), np.concatenate([q[1] for q in qs], axis=1))
def put(q, e, v):
    c, s = q[0].reshape(128, -1, 4).copy(), q[1].copy(); c[:, e] = v[0].reshape(128, -1, 4); s[:, e] = v[1]
    return (c.reshape(128, -1), s)
def pk(c, s):
    return (np.ascontiguousarray(c), mx_ref.live(s))
def emit(q):
    return q[0], q[1]
def packed(v, rng):
    q = [mx_ref.quantize(np.ascontiguousarray(v[r])) for r in range(N)]
    return np.stack([a for a, b in q]), np.stack([mx_ref.plane(b, rng) for a, b in q])
def values_of_codes():
    e, c = np.zeros((128, 128, 4), np.float32), np.zeros((128, 2, 4), np.uint8)
    e[np.arange(128), np.arange(128), 0] = 1
    c[:127, :, 0] = np.arange(256).reshape(2, 128).T[:127]
    return mx_ref.matmul(mx_ref.quantize(e.reshape(128, 512).astype(BF)), (c.reshape(128, 8), np.full((16, 2), 127, np.uint8))).T.reshape(-1).astype(np.float64)
CODE_VALUE, SCALE_VALUE = values_of_codes(), 2.0 ** (np.arange(256) - 127.0)
def decode(q):
    return (CODE_VALUE[q[0]].reshape(16, 8, -1, 4) * SCALE_VALUE[q[1]][:, None, :, None] + 0.0).reshape(128, -1).astype(np.float32)
def f(rng, *shape):
    return mx_ref.flush((rng.standard_normal(shape, dtype=np.float32) * np.exp2(rng.integers(-2, 3, shape[:-1] + (1,)))).astype(BF))
def wide(rng, *shape, cols=0):
    v = rng.standard_normal(shape, dtype=np.float32) * np.exp2(rng.integers(-12, 13, shape)).astype(np.float32)
    if cols: v *= np.repeat(np.exp2(rng.integers(-cols, cols + 1, shape[:-2] + (1, shape[-1] // 4))) * (rng.random(shape[:-2] + (1, shape[-1] // 4)) > 0.0625), 4, axis=-1).astype(np.float32)
    return mx_ref.flush(v.astype(BF))
C, H = 384, 192
STEP = [4, 1, 2]
def numbers_of(rng):
    return {"x": np.array(f(rng, N, 128, 4 * C)), "u": np.array(f(rng, N, 128, 512)), "v": np.array(f(rng, N, 128, 512))}
def stored(k):
    return {"nl": np.stack([gtable(k[r]) for r in range(N)])}
def lists(rng):
    return stored(rng.permuted(np.tile(np.arange(C), (N, 8, 1)), axis=2))
def layers(rng, still=()):
    w = np.array(f(rng, N, 128, 2048)).reshape(N, 8, 16, 4, 8, 16, 4)
    for i in still:
        w[:, :, i] = 0
        w[:, :, :, :, :, i] = 0
    return w
def weights(rng, w):
    c, p = packed(np.ascontiguousarray(w).reshape(N, 128, 2048), rng)
    return {"wc": c, "ws": p}
def setup_inputs(rng):
    return {**numbers_of(rng), **lists(rng), **weights(rng, layers(rng))}
def setup_inputs_ties(rng):
    d = numbers_of(rng)
    o = rng.permutation(N)
    k = rng.integers(-1, 2, (N, 8, 3, C)).astype(np.float32)
    k[o[1]] = 1
    x = d["x"].reshape(N, 8, 16, C, 4)
    x[:, :, :3] = 0
    x[:, :, :3, :, 0] = k.astype(BF)
    c = np.ones(N, np.float32)
    c[o[0]] = 0
    c[o[2]] = -1
    u = d["u"].reshape(N, 8, 16, 8, 16, 4)
    u[:, :, :, :, :3] = 0
    g = np.arange(8)
    for j in range(3): u[:, g, j, g, j, 0] = c.astype(BF)[:, None]
    w = layers(rng)
    w[:, :, :, :, :, :8] = 0
    return {"x": x.reshape(N, 128, 4 * C), "u": u.reshape(N, 128, 512), "v": d["v"], **lists(rng), **weights(rng, w)}
def setup_inputs_near(rng):
    d = numbers_of(rng)
    o = rng.permutation(N) % 3
    x = d["x"].astype(np.float32).reshape(N, 8, 16, C, 4)
    u = d["u"].astype(np.float32).reshape(N, 8, 16, 8, 16, 4)
    w = layers(rng, range(8))
    x[:, :, :8] = 0
    u[:, :, :, :, :3] = 0
    g = np.arange(8)
    for r in range(N):
        k, e = (1.0, 1.0) if o[r] == 0 else (2.0 ** -28, 2.0 ** -30)
        if o[r] == 2:
            x[r, :, 8:] = 0
            x[r, :, 8, :, 0] = k
            w[r] = 0
        for j in range(3):
            u[r, g, 6, g, j, 0] = e
            if o[r] < 2:
                s = rng.integers(-1, 2, (8, C)) * k
                x[r, :, 2 * j, :, 0] = 1.125 * s
                x[r, :, 2 * j + 1, :, 0] = -1.25 * s
                u[r, g, 2 * j, g, j, 0] = 1.125 * e
                u[r, g, 2 * j + 1, g, j, 0] = e
            else:
                x[r, :, 9 + j, :, 0] = k * rng.choice([-1.0, 1.0], (8, C))
                u[r, g, 12 + j, g, j, 0] = e
                w[r, g, 9 + j, 0, g, 12 + j, 0] = 2.0 ** -8
        at = [0, C - 1, int(rng.integers(C)), int(rng.integers(C))]
        for h, c in zip(rng.permutation(8)[:4], at): x[r, h, 6, c, 0] = 2.0 ** 30 * rng.choice([-1.0, 1.0])
    return {"x": x.reshape(N, 128, 4 * C).astype(BF), "u": u.reshape(N, 128, 512).astype(BF), "v": d["v"], **lists(rng), **weights(rng, w)}
def setup_inputs_odd(rng):
    d = numbers_of(rng)
    x = (1.0 + (2 * rng.integers(0, 64, (N, 16, 8, C, 4)) + 1) * 2.0 ** -7) * np.exp2(-rng.integers(0, 7, (N, 16, 8, C, 4)).astype(np.float64)) * rng.choice([-1.0, 1.0], (N, 16, 8, C, 4))
    x[:, :, 0, :, 0] = 1.96875 * 2.0 ** 8 * rng.choice([-1.0, 1.0], (N, 16, 1))
    u = d["u"].reshape(N, 16, 8, 128, 4)
    u[:, :, 0] = 0
    return {"x": x.astype(np.float32).reshape(N, 128, 4 * C).astype(BF), "u": u.reshape(N, 128, 512), "v": d["v"], **lists(rng), **weights(rng, layers(rng, (0, 8)))}
def setup_inputs_ends(rng):
    d = numbers_of(rng)
    o, e = rng.permutation(N) % 4, rng.permutation(N) % 4
    x = np.zeros((N, 8, 16, C, 4))
    u = d["u"].astype(np.float32).reshape(N, 8, 16, 8, 16, 4)
    v = d["v"].astype(np.float32)
    w = np.zeros((N, 8, 16, 4, 8, 16, 4), np.float32)
    k = np.tile(np.arange(C), (N, 8, 1))
    def sized(small, low, *q):
        return (1.0 + 0.125 * rng.integers(0, 8, q)) * 2.0 ** -30 if small else (low + 0.1 * rng.random(q)) * 2.0 ** 30
    for r in range(N):
        h = rng.permutation(8)
        c = np.where(h < 2, 0.0, h % 2 * 2.0 - 1.0)[:, None] * np.where((h > 5)[:, None], [1.0, -1.0, 1.0], 1.0)
        c = c[None, None, :, :, None]
        if o[r] == 3:
            x[r] = d["x"][r].astype(np.float32).reshape(8, 16, C, 4)[:, :, :1]
            u[r, :, :, :, :3] *= np.abs(c).astype(np.float32)
        else:
            small = o[r] == 2
            x[r] = sized(small, 0.7, 8, 16, C, 4) * (rng.choice([-1.0, 1.0], (C, 1)) if o[r] == 1 else -1.0)
            u[r, :, :, :, :3] = c * sized(small, 0.9, 8, 16, 8, 3, 4)
            v[r] = sized(small, 0.9, 128, 512) * rng.choice([-1.0, 1.0], (128, 512))
        if o[r] != 2: x[r, :, 14:] = 0
        i, last = np.arange(14), np.arange(14, 16)
        for g in range(8):
            for b in range(4):
                w[r, g, i, b, g, i, b] = 2.0 ** -8 if o[r] == 3 else 2.0
                if o[r] == 2: w[r, g, last, b, g, last, b] = 256.0
        if e[r] == 1: k[r] = C - 1 - np.arange(C)
        if e[r] == 2:
            k[r, :, :H] = 2 * np.arange(H)
            k[r, :, H:] = 2 * np.arange(H)[::-1] + 1
        if e[r] == 3: k[r] = rng.permuted(k[r], axis=1)
    return {"x": x.astype(np.float32).reshape(N, 128, 4 * C).astype(BF), "u": u.reshape(N, 128, 512).astype(BF), "v": v.astype(BF), **stored(k), **weights(rng, w.astype(BF))}
def setup_inputs_spread(rng):
    d = setup_inputs(rng)
    d["x"] = wide(rng, N, 128, 4 * C, cols=6)
    return d
def check_inputs(d):
    b = []
    for k in ("x", "u", "v"):
        a = np.abs(d[k].astype(np.float32))
        if not (np.isfinite(a).all() and ((a == 0) | (a >= 2.0 ** -30) & (a <= 2.0 ** 30)).all()): b.append("a value of " + k)
    none, least, most = [emit(mx_ref.quantize(np.full((128, 16), k, np.float32).astype(BF)))[1][0, 0] for k in (0.0, 2.0 ** -8, 2.0 ** 8)]
    for r in range(N):
        if (np.sort(gentries(d["nl"][r]), axis=1) != np.arange(C)).any(): b.append("nl: a list that is no permutation")
        if ((d["wc"][r] == 0x7F) | (d["wc"][r] == 0xFF)).any(): b.append("wc: a code that is no number")
        s = mx_ref.live(d["ws"][r])
        if ((s != none) & ((s < least) | (s > most))).any(): b.append("ws: a scale out of range")
        if (((d["wc"][r].reshape(16, 8, 512, 4) & 0x7F) != 0) & (s == none)[:, None, :, None]).any(): b.append("wc: a code other than zero under the scale of zeros")
    return b
def ends(n):
    return np.take_along_axis(np.argsort(n, axis=1), n ^ 1, axis=1)
def reference(x, u, v, nl, wc, ws):
    qu = [mx_ref.quantize(u[r]) for r in range(N)]
    lay = [pk(wc[r], ws[r]) for r in range(N)]
    name = [gentries(nl[r]).astype(np.int64) for r in range(N)]
    now = [x[r] for r in range(N)]
    for step in STEP:
        z = []
        for r in range(N):
            s = mx_ref.matmul(qu[r], mx_ref.quantize(now[r])).reshape(8, 16, C)
            for j in range(3):
                d = ends(name[r])
                h = np.where(name[r] % 2 == 0, np.arange(C), d)
                flag = np.take_along_axis(s[:, j], h, axis=1) > 0
                then = np.roll(name[r], -1, axis=0)
                name[r] = np.roll(np.where(flag, np.take_along_axis(then, d, axis=1), then), 1, axis=0)
            z.append(((gcols(now[r], name[r]).astype(np.float32) + gcols(now[r], ends(name[r])).astype(np.float32)) * np.float32(0.5)).astype(BF))
        made = []
        for r in range(N):
            p = (r - step) % N
            m = np.take_along_axis(np.argsort(name[p], axis=1), name[r], axis=1)
            far = gcols(decode(mx_ref.quantize(z[p])).astype(BF), m[:, :H])
            q = mx_ref.quantize(np.ascontiguousarray(np.concatenate([far, gcols(z[r], m[:, H:])], axis=1)))
            made.append(tile([now[r][:, b::4].astype(np.float32) + mx_ref.matmul(pick(lay[r], np.arange(128 * b, 128 * b + 128)), q) * np.float32(0.03125) for b in range(4)]))
        now = made
    y, nm = np.zeros((N, 128, C), np.float32), np.zeros((N, 8, C), np.float32)
    oc, osc = np.zeros((N, 128, 4 * C), np.uint8), np.zeros((N, 16, C), np.uint8)
    for r in range(N):
        q = mx_ref.quantize(now[r])
        y[r] = mx_ref.matmul(mx_ref.quantize(v[r]), q)
        nm[r] = name[r]
        oc[r], osc[r] = emit(q)
    return {"y": y, "nm": nm, "oc": oc, "osc": osc}

@@ -1,0 +1,406 @@
+from concourse.bass import DstId, RemoteDMATransfer
+from concourse.mybir import dt, AluOpType, ActivationFunctionType
+
+C, H, N = 384, 192, 8
+ROUNDS = 3
+STEPS = [4, 1, 2]
+PARTS = ((0, 256), (256, 384))
+
+SCRATCH = {
+    "xt": ("sbuf", [128, 1536], "bfloat16"), "yb": ("sbuf", [128, 1536], "bfloat16"),
+    "xh": ("sbuf", [128, 1536], "bfloat16"), "xg": ("sbuf", [128, 1536], "bfloat16"),
+    "qx": ("sbuf", [128, 384], "float8_e4m3fn_x4"), "sx": ("sbuf", [128, 384], "uint8"),
+    "ua": ("sbuf", [128, 520], "bfloat16"), "ub": ("sbuf", [128, 512], "bfloat16"), "vt": ("sbuf", [128, 512], "bfloat16"),
+    "qua": ("sbuf", [128, 130], "float8_e4m3fn_x4"), "sua": ("sbuf", [128, 130], "uint8"),
+    "qub": ("sbuf", [128, 128], "float8_e4m3fn_x4"), "sub": ("sbuf", [128, 128], "uint8"),
+    "qvt": ("sbuf", [128, 128], "float8_e4m3fn_x4"), "svt": ("sbuf", [128, 128], "uint8"),
+    "wq": ("sbuf", [128, 512], "float8_e4m3fn_x4"), "wp": ("sbuf", [128, 512], "uint8"),
+    "nlb": ("sbuf", [128, 48], "int32"), "nla": ("sbuf", [128, 192], "int32"), "pn": ("sbuf", [128, 48], "uint16"),
+    "kk": ("sbuf", [128, 144], "int32"), "clu": ("sbuf", [128, 6], "uint16"), "oe": ("sbuf", [128, 32], "uint16"),
+    "ci": ("sbuf", [128, 384], "bfloat16"), "nmt": ("sbuf", [128, 384], "float32"),
+    "one": ("sbuf", [128, 2048], "bfloat16"), "et": ("sbuf", [128, 2048], "bfloat16"),
+    "qe": ("sbuf", [128, 512], "float8_e4m3fn_x4"), "se": ("sbuf", [128, 512], "uint8"),
+    "f0": ("sbuf", [128, 384], "bfloat16"), "f1": ("sbuf", [128, 384], "bfloat16"), "f2": ("sbuf", [128, 384], "bfloat16"),
+    "sg1": ("sbuf", [128, 384], "bfloat16"), "sg2": ("sbuf", [128, 384], "bfloat16"),
+    "li0": ("sbuf", [128, 400], "bfloat16"), "li1": ("sbuf", [128, 400], "bfloat16"),
+    "pp": ("sbuf", [128, 384], "float32"), "dl": ("sbuf", [128, 384], "float32"),
+    "tt": ("sbuf", [128, 1536], "bfloat16"), "td": ("sbuf", [128, 192], "float32"), "dd": ("sbuf", [128, 192], "float32"),
+    "zn": ("sbuf", [128, 1536], "bfloat16"), "nu": ("sbuf", [128, 400], "bfloat16"), "nmu": ("sbuf", [128, 384], "float32"),
+    "tn": ("sbuf", [128, 768], "bfloat16"), "te": ("sbuf", [128, 768], "bfloat16"),
+    "bw": ("sbuf", [128, 384], "bfloat16"), "eu": ("sbuf", [128, 400], "bfloat16"), "ew": ("sbuf", [128, 64], "uint16"),
+    "dn": ("sbuf", [128, 1536], "bfloat16"), "vo": ("sbuf", [128, 768], "bfloat16"), "vf": ("sbuf", [128, 768], "bfloat16"),
+    "qvo": ("sbuf", [128, 192], "float8_e4m3fn_x4"), "svo": ("sbuf", [128, 192], "uint8"),
+    "qvf": ("sbuf", [128, 192], "float8_e4m3fn_x4"), "svf": ("sbuf", [128, 192], "uint8"),
+    "ysb": ("sbuf", [128, 384], "float32"),
+    "pa": ("psum", [128, 2048], "float32"), "pb": ("psum", [128, 2048], "float32"),
+}
+for _r in range(ROUNDS):
+    SCRATCH["nw%d" % _r] = ("sbuf", [128, 32], "uint16")
+    SCRATCH["ip%d" % _r] = ("sbuf", [128, 24], "uint16")
+    SCRATCH["qz%d" % _r] = ("sbuf", [128, 384], "float8_e4m3fn_x4")
+    SCRATCH["sz%d" % _r] = ("sbuf", [128, 384], "uint8")
+    SCRATCH["lq%d" % _r] = ("sbuf", [128, 384], "float8_e4m3fn_x4")
+    SCRATCH["lz%d" % _r] = ("sbuf", [128, 384], "uint8")
+for _r in range(3 * ROUNDS + 1):
+    SCRATCH["iw%d" % _r] = ("sbuf", [128, 64], "uint16")
+
+SEMAPHORES = ["cV", "cS", "cP", "cG", "sent"] + ["d%d" % k for k in range(24)] \
+    + ["al%d" % k for k in range(ROUNDS)] + ["az%d" % k for k in range(2 * ROUNDS)]
+
+
+def rank_program(g, core, T, topo):
+    rank = T.rank_of(core)
+    if rank is None:
+        return
+    A = AluOpType
+    Copy, Sign, Relu = ActivationFunctionType.Copy, ActivationFunctionType.Sign, ActivationFunctionType.Relu
+
+    queue = {"V": g.vector, "S": g.scalar, "P": g.tensor, "G": g, "Y": g.sync}
+    known = {q: {} for q in queue}
+    done = {}
+    total = {}
+    acc = {}
+    ndma = [0]
+
+    def gcd(a, b):
+        while b:
+            a, b = b, a % b
+        return a
+
+    def meets(a, b):
+        if a[2] <= b[1] or b[2] <= a[1]:
+            return False
+        return (a[1] - b[1]) % gcd(a[3], b[3]) == 0
+
+    def norm(k):
+        return (k, 0, 1 << 20, 1) if isinstance(k, str) else tuple(k) + (1,) * (4 - len(k))
+
+    def wait(q, toks):
+        best = {}
+        for s, v in toks:
+            if known[q].get(s, 0) < v:
+                best[s] = max(best.get(s, 0), v)
+        need = list(best.items())
+        keep = [t for t in need if not any(o != t and done.get(o, {}).get(t[0], 0) >= t[1] for o in need)]
+        for s, v in keep:
+            queue[q].wait_ge(T.sem[s], v)
+            for a, b in list(done.get((s, v), {}).items()) + [(s, v)]:
+                known[q][a] = max(known[q].get(a, 0), b)
+
+    def note(tok, reads, writes):
+        for w, ks in ((False, reads), (True, writes)):
+            for k in ks:
+                n = norm(k)
+                lst = acc.setdefault(n[0], [])
+                if w and n[3] == 1:
+                    lst[:] = [e for e in lst if not (n[1] <= e[1] and e[2] <= n[2])]
+                lst.append((tok, n[1], n[2], n[3], w))
+
+    def op(q, fn, reads=(), writes=(), dma=False):
+        toks = []
+        for w, ks in ((False, reads), (True, writes)):
+            for k in ks:
+                n = norm(k)
+                for e in acc.get(n[0], ()):
+                    if (w or e[4]) and meets(e, n):
+                        toks.append(e[0])
+        wait(q, toks)
+        if dma:
+            s, v = "d%d" % ndma[0], 16
+            ndma[0] += 1
+            total[s] = v
+            fn(queue[q]).then_inc(T.sem[s], 16)
+        else:
+            s = "c" + q
+            total[s] = v = total.get(s, 0) + 1
+            fn(queue[q]).then_inc(T.sem[s], 1)
+        done[(s, v)] = dict(known[q])
+        note((s, v), reads, writes)
+
+    def bank(j):
+        return (T.pa if j < 4 else T.pb), 512 * (j % 4), "bank%d" % j
+
+    def mm(j, n, lq, ls, la, rq, rs, ra):
+        buf, o, key = bank(j)
+        op("P", lambda e: e.matmul_mx(buf[:, o:o + n], T[lq][:, la:la + 128], T[ls][:, la:la + 128],
+                                      T[rq][:, ra:ra + n], T[rs][:, ra:ra + n], True, True),
+           [(lq, la, la + 128), (ls, la, la + 128), (rq, ra, ra + n)], [key])
+
+    def quant(q, s, src, a, n, t=0):
+        op("V", lambda e: e.quantize_mx(T[q][:, a:a + n], T[s][:, a:a + n], T[src][:, t:t + 4 * n]),
+           [(src, t, t + 4 * n)], [(q, a, a + n)])
+
+    def ts(out, i, s1, s2, o0, o1, reads, writes):
+        if o1 is None:
+            op("V", lambda e: e.tensor_scalar(out, i, s1, None, o0), reads, writes)
+        else:
+            op("V", lambda e: e.tensor_scalar(out, i, s1, s2, o0, o1), reads, writes)
+
+    def tt(out, a, b, o, reads, writes):
+        op("V", lambda e: e.tensor_tensor(out, a, b, o), reads, writes)
+
+    def cp(out, a, reads, writes):
+        op("V", lambda e: e.tensor_copy(out, a), reads, writes)
+
+    def act(out, a, fn, reads, writes, scale=1.0):
+        op("S", lambda e: e.activation(out, a, fn, scale=scale), reads, writes)
+
+    def copy_on(q, out, a, reads, writes):
+        if q == "V":
+            cp(out, a, reads, writes)
+        else:
+            act(out, a, Copy, reads, writes)
+
+    def load(q, out, src, key):
+        op(q, lambda e: e.dma_start(out, src), [], [key], dma=True)
+
+    def iota(buf, pattern, base, key, cm=0, a=None):
+        out = T[buf][:, :] if a is None else T[buf][:, a[0]:a[1]]
+        if buf == "kk":
+            op("G", lambda e: e.iota(out, pattern, base, cm), [], [key])
+        else:
+            op("G", lambda e: e.iota(out, pattern, base, cm, allow_small_or_imprecise_dtypes=True), [], [key])
+
+    shifted = ["tsh%d" % a for a in range(4)]
+    load("Y", T.nlb[0:112, 24:48], T.nl[16:128, :], "nlb.a")
+    load("S", T.nlb[112:128, 24:48], T.nl[0:16, :], "nlb.b")
+    load("Y", T.nlb[:, 0:24], T.nl[:, :], "nlb.c")
+    load("S", T.xt[:, :], T.x[:, :], ("xt", 0, 1536))
+    load("Y", T.ua[:, 0:512], T.u[:, :], ("ua", 0, 512))
+    load("Y", T.ua[:, 512:520], T.u[:, 0:8], ("ua", 512, 520))
+    load("Y", T.ub[:, 0:508], T.u[:, 4:512], ("ub", 0, 508))
+    load("Y", T.ub[:, 508:512], T.u[:, 0:4], ("ub", 508, 512))
+    load("Y", T.wq[:, :].bitcast(dt.uint8), T.wc[:, :], ("wq", 0, 512))
+    load("Y", T.wp[:, :], T.ws[:, :], ("wp", 0, 512))
+    load("Y", T.vt[:, :], T.v[:, :], ("vt", 0, 512))
+
+    iota("kk", [[0, 6]], 0, ("kk", 0, 6), 1, (0, 6))
+    iota("kk", [[16, 6]], 0, ("kk", 6, 12), 0, (6, 12))
+    iota("ci", [[1, 384]], -192, "ci")
+    op("G", lambda e: e.iota(T.tt[:, :], [[0, 1536]], 0, 0, allow_small_or_imprecise_dtypes=True), [], ["tt"] + shifted)
+    iota("tn", [[0, 768]], 0, "tn")
+    iota("te", [[0, 768]], 0, "te")
+    iota("eu", [[0, 400]], 0, "eu")
+    iota("one", [[0, 2048]], 1, "one")
+    op("G", lambda e: e.affine_select(T.et[:, :], T.one[:, :], [[-1, 4], [1, 512]], A.is_equal, 0.0, 0, -4), ["one"], ["et"])
+    op("V", lambda e: e.memset(T.td[:, :], 0.0), [], ["td"])
+
+    def kc(i):
+        return T.kk[:, 6 * i:6 * i + 6]
+
+    def kr(*i):
+        return [("kk", 6 * j, 6 * j + 6) for j in i]
+    ts(kc(2), kc(0), 15, None, A.bitwise_and, None, kr(0), kr(2))
+    ts(kc(3), kc(0), 4, 1, A.logical_shift_right, A.bitwise_and, kr(0), kr(3))
+    tt(kc(4), kc(2), kc(1), A.add, kr(2, 1), kr(4))
+    ts(kc(17), kc(3), -784, 768, A.mult, A.add, kr(3), kr(17))
+    ts(kc(5), kc(4), 31, None, A.bitwise_and, None, kr(4), kr(5))
+    ts(kc(18), kc(4), 32, None, A.is_lt, None, kr(4), kr(18))
+    ts(kc(20), kc(4), 64, 12, A.is_ge, A.mult, kr(4), kr(20))
+    ts(kc(21), kc(4), 64, None, A.is_ge, None, kr(4), kr(21))
+    tt(kc(22), kc(5), kc(20), A.add, kr(5, 20), kr(22))
+    tt(kc(23), kc(18), kc(21), A.add, kr(18, 21), kr(23))
+    ts(kc(6), kc(22), 24, -24, A.is_ge, A.mult, kr(22), kr(6))
+    tt(kc(19), kc(17), kc(23), A.mult, kr(17, 23), kr(19))
+    tt(kc(7), kc(22), kc(6), A.add, kr(22, 6), kr(7))
+    tt(kc(8), kc(7), kc(3), A.add, kr(7, 3), kr(8))
+    ts(kc(10), kc(7), 0, 384, A.is_equal, A.mult, kr(7), kr(10))
+    ts(kc(12), kc(7), 16, None, A.mult, None, kr(7), kr(12))
+    ts(kc(9), kc(8), 1, None, A.bitwise_and, None, kr(8), kr(9))
+    tt(kc(11), kc(10), kc(3), A.mult, kr(10, 3), kr(11))
+    ts(kc(13), kc(9), 368, None, A.mult, None, kr(9), kr(13))
+    tt(kc(14), kc(11), kc(19), A.add, kr(11, 19), kr(14))
+    tt(kc(15), kc(12), kc(13), A.add, kr(12, 13), kr(15))
+    tt(kc(16), kc(14), kc(15), A.add, kr(14, 15), kr(16))
+    cp(T.clu[:, :], kc(16), kr(16), ["clu"])
+
+    nl = ["nlb.a", "nlb.b", "nlb.c"]
+    ts(T.nla[:, 0:48], T.nlb[:, :], 1, None, A.bitwise_and, None, nl, [("nla", 0, 48)])
+    ts(T.nla[:, 48:96], T.nlb[:, :], 1, None, A.logical_shift_right, None, nl, [("nla", 48, 96)])
+    ts(T.nla[:, 96:144], T.nla[:, 0:48], 192, None, A.mult, None, [("nla", 0, 48)], [("nla", 96, 144)])
+    tt(T.nla[:, 144:192], T.nla[:, 48:96], T.nla[:, 96:144], A.add, [("nla", 48, 144)], [("nla", 144, 192)])
+    cp(T.pn[:, :], T.nla[:, 144:192], [("nla", 144, 192)], ["pn"])
+    cp(T.li0[:, 0:384].indirect(T.pn[:, 24:48]), T.ci[:, :], ["pn", "ci"], [("li0", 0, 384)])
+    cp(T.li0[:, 384:400], T.li0[:, 0:16], [("li0", 0, 16)], [("li0", 384, 400)])
+    quant("qua", "sua", "ua", 0, 130)
+    quant("qx", "sx", "xt", 0, 384)
+
+    def transposes(dst, src, parts):
+        for o, a, n in parts:
+            op("V", lambda e: e.transpose(T[dst][:, o:o + n], T[src][:, a:a + n]), [(src, a, a + n)], [(dst, o, o + n)])
+
+    def move():
+        for a in range(4):
+            b = (a + 1) % 4
+            cp(T.tt[32 * b:32 * b + 32, 768:1536:32], T.tt[32 * a:32 * a + 32, 16:768:32], [("tt", 0, 768)], ["tsh%d" % b])
+
+    def tables(k):
+        ts(T["iw%d" % k][:, 0:64], T.tt[:, 0:1536].indirect(T.clu[:, 0:4]), 192.0, None, A.add, None,
+           [("tt", 0, 768), "clu"] + shifted, ["iw%d" % k])
+
+    def diff_same():
+        tt(T.td[:, 16:192:32], T.tt[:, 192:384:32], T.tt[:, 0:192:32], A.subtract, [("tt", 0, 384)], [("td", 16, 192, 32)])
+
+    def diff_next():
+        tt(T.td[:, 0:192:32], T.tt[:, 960:1152:32], T.tt[:, 768:960:32], A.subtract, shifted, [("td", 0, 192, 32)])
+
+    def diff_back():
+        op("V", lambda e: e.transpose(T.dd[:, :], T.td[:, :]), [("td", 0, 192)], ["dd"])
+
+    def wrap(src, k, diffs):
+        transposes("tt", src, [(0, 0, 384), (384, 16, 384)])
+        if diffs:
+            diff_same()
+        move()
+        if diffs:
+            diff_next()
+            tables(k)
+            diff_back()
+        else:
+            ts(T.oe[:, :], T.tt[:, 0:1536].indirect(T.clu[:, 4:6]), 192.0, None, A.add, None,
+               [("tt", 0, 768), "clu"] + shifted, ["oe"])
+
+    def send(dst, out, src, sem):
+        rid, pid = topo.addr(dst, core)
+        g.remote_dma(out, src, T.sem[sem], T.sem.sent, pid, rid, topo.mask(core, dst))
+        total["sent"] = total.get("sent", 0) + len(topo.engines(core, dst))
+
+    wrap("li0", 0, True)
+    cur, li = 0, 0
+    for r in range(ROUNDS):
+        last = r == ROUNDS - 1
+        to, frm = T.cores[(rank + STEPS[r]) % N], T.cores[(rank - STEPS[r]) % N]
+        nin = len(topo.engines(frm, core))
+        own = "pn" if r == 0 else "nw%d" % (r - 1)
+        nw, qz, sz, lq, lz, ip = ("%s%d" % (k, r) for k in ("nw", "qz", "sz", "lq", "lz", "ip"))
+        n = 384 if r == 0 else 192
+        mm(0, n, "qua", "sua", 0, "qx", "sx", 0)
+        ts(T.f0[:, 0:n], T.pa[:, 0:n], 0.0, None, A.is_gt, None, ["bank0"], [("f0", 0, n), "bank0"])
+        if r == 0:
+            quant("qub", "sub", "ub", 0, 128)
+        mm(1, 384, "qub", "sub", 0, "qx", "sx", 0)
+        mm(2, 384, "qua", "sua", 2, "qx", "sx", 0)
+
+        def beside(j):
+            if j == 0:
+                for k in (1, 2):
+                    act(T["sg%d" % k][:, :], T.pa[:, 512 * k:512 * k + 384], Sign, ["bank%d" % k], ["sg%d" % k, "bank%d" % k])
+                    act(T["f%d" % k][:, :], T["sg%d" % k][:, :], Relu, ["sg%d" % k], ["f%d" % k])
+            for t in ((0, 1), (2, 3), ())[j]:
+                act(T.xh[:, 384 * t:384 * t + 384], T.xt[:, t:1536:4], Copy, [("xt", t, 1536, 4)],
+                    [("xh", 384 * t, 384 * t + 384)], scale=0.5)
+            if j == 1:
+                for t in range(4):
+                    for h in range(2):
+                        o = 384 * t + 192 * h
+                        act(T.xg[:, o:o + 192], T.xt[:, 4 * h + t:1536:8], Copy, [("xt", 4 * h + t, 1536, 8)],
+                            [("xg", o, o + 192)], scale=0.5)
+            if j == 2 and r == 0:
+                act(T.yb[:, :], T.xt[:, :], Copy, [("xt", 0, 1536)], [("yb", 0, 1536)], scale=32.0)
+        for j in range(3):
+            iw, f, lo, ln = "iw%d" % cur, "f%d" % j, "li%d" % li, "li%d" % (1 - li)
+            tt(T.pp[:, 0:192], T[f][:, 0:384].indirect(T[iw][:, 0:12]), T.dd[:, :], A.mult, [f, iw, "dd"], [("pp", 0, 192)])
+            if j == 0:
+                ts(T.pp[:, 192:384], T.pp[:, 0:192], -1.0, None, A.mult, None, [("pp", 0, 192)], [("pp", 192, 384)])
+                act(T.dl[:, 192:384], T.pp[:, 0:384].indirect(T[own][:, 12:24]), Copy, [("pp", 0, 384), own], [("dl", 192, 384)])
+                cp(T.dl[:, 0:192], T.pp[:, 0:384].indirect(T[own][:, 0:12]), [("pp", 0, 384), own], [("dl", 0, 192)])
+            else:
+                act(T.pp[:, 192:384], T.pp[:, 0:192], Copy, [("pp", 0, 192)], [("pp", 192, 384)], scale=-1.0)
+                for h in range(2):
+                    cp(T.dl[:, 0:384].indirect(T[iw][:, 12 * h:12 * h + 12]), T.pp[:, 192 * h:192 * h + 192],
+                       [("pp", 192 * h, 192 * h + 192), iw], ["dl"])
+            tt(T[ln][:, 0:400], T.dl[:, 0:384].indirect(T[iw][:, 32:57]), T[lo][:, 0:400], A.add,
+               ["dl", iw, (lo, 0, 400)], [(ln, 0, 400)])
+            beside(j)
+            li, cur = 1 - li, cur + 1
+            wrap(ln, cur, j < 2)
+        iw = "iw%d" % cur
+        for h, (a, b) in enumerate(PARTS):
+            az = "az%d" % (2 * r + h)
+            for t in range(4):
+                tt(T.zn[:, 4 * a + t:4 * b:4], T.xh[:, 384 * t:384 * t + 384].indirect(T.oe[:, a // 16:b // 16]),
+                   T.xg[:, 384 * t + a:384 * t + b], A.add, [("xh", 384 * t, 384 * t + 384), ("xg", 384 * t, 384 * t + 384), "oe"],
+                   [("zn", 4 * a + t, 4 * b, 4)])
+                if h == 0 and t == 0:
+                    tables(cur)
+                    wait("G", [acc[iw][0][0]])
+                    send(to, T[ip][:, 0:24], T[iw][:, 0:24], "al%d" % r)
+                    note(("al%d" % r, nin), [], [ip])
+                    total["al%d" % r] = nin
+            quant(qz, sz, "zn", a, b - a, 4 * a)
+            wait("G", [("cV", total["cV"])])
+            send(to, T[lq][:, a:b].bitcast(dt.uint8), T[qz][:, a:b].bitcast(dt.uint8), az)
+            send(to, T[lz][:, a:b], T[sz][:, a:b], az)
+            total[az] = 2 * nin
+            note((az, 2 * nin), [], [(lq, a, b)])
+        if r == 0:
+            iota("nmt", [[1, 2], [2, 192]], 0, "nmt")
+        cp(T.nu[:, 0:384].indirect(T[iw][:, 0:24]), T.ci[:, :], [iw, "ci"], [("nu", 0, 384)])
+        cp(T.nu[:, 384:400], T.nu[:, 0:16], [("nu", 0, 16)], [("nu", 384, 400)])
+        transposes("tn", "nu", [(0, 0, 384), (384, 16, 384)])
+        ts(T[nw][:, 0:32], T.tn[:, 0:768].indirect(T.clu[:, 2:4]), 192.0, None, A.add, None, ["tn", "clu"], [nw])
+        act(T.bw[:, :], T.nu[:, 0:384].indirect(T[ip][:, 0:24]), Copy, [("nu", 0, 384), ip], ["bw"])
+        act(T.eu[:, 0:192], T.bw[:, 0:384].indirect(T[nw][:, 12:24]), Copy, ["bw", nw], [("eu", 0, 192)])
+        act(T.eu[:, 384:400], T.eu[:, 0:16], Copy, [("eu", 0, 16)], [("eu", 384, 400)])
+        if not last:
+            diff_same()
+            diff_next()
+            diff_back()
+        else:
+            cp(T.nmu[:, 0:384].indirect(T[iw][:, 0:24]), T.nmt[:, :], [iw, "nmt"], ["nmu"])
+            op("Y", lambda e: e.dma_start(T.nm[:, :], T.nmu[0:128:16, :]), ["nmu"], [], dma=True)
+        if r == 0:
+            quant("qe", "se", "et", 0, 512)
+            quant("qvt", "svt", "vt", 0, 128)
+        transposes("te", "eu", [(0, 0, 192), (384, 16, 192), (736, 368, 32)])
+        for t in (2, 3, 0, 1):
+            ts(T.ew[:, 16 * t:16 * t + 16], T.te[:, 0:768].indirect(T.clu[:, 2:3]), 4.0, 768.0 + t, A.mult, A.add,
+               ["te", "clu"], [("ew", 16 * t, 16 * t + 16)])
+        for t in (2, 0, 3, 1):
+            copy_on("VVSS"[t], T.vo[:, t:768:4], T.zn[:, 0:1536].indirect(T.ew[:, 16 * t:16 * t + 12]),
+                    [("zn", 0, 1536), ("ew", 16 * t, 16 * t + 16)], [("vo", t, 768, 4)])
+        quant("qvo", "svo", "vo", 0, 192)
+        for b in range(4):
+            mm(b, 192, "wq", "wp", 128 * b, "qvo", "svo", 0)
+
+        def renew(first, o):
+            for b in range(4):
+                buf, c, key = bank(first + b)
+                y = T.yb[:, o + b:o + 768:4]
+                tt(y, buf[:, c:c + 192], y, A.add, [key, ("yb", o + b, o + 768, 4)], [key, ("yb", o + b, o + 768, 4)])
+                k = ([("yb", o + b, o + 768, 4)], [("xt", o + b, o + 768, 4)])
+                if b < 3:
+                    act(T.xt[:, o + b:o + 768:4], y, Copy, *k, scale=2.0 ** -5)
+                else:
+                    ts(T.xt[:, o + b:o + 768:4], y, 2.0 ** -5, None, A.mult, None, *k)
+            quant("qx", "sx", "xt", o // 4, 192, o)
+        renew(0, 768)
+        if last:
+            op("Y", lambda e: e.dma_start(T.oc[:, 768:1536], T.qx[:, 192:384].bitcast(dt.uint8)), [("qx", 192, 384)], [], dma=True)
+        for h, (p, e) in enumerate(PARTS):
+            for b in (1, 2, 3, 0):
+                mm(b if h else 4 + b, e - p, "qe", "se", 128 * b, lq, lz, p)
+            if h == 0:
+                mm(0, 192, "qvt" if last else "qua", "svt" if last else "sua", 0, "qx", "sx", 192)
+            for b in (1, 2, 3, 0):
+                buf, c, key = bank(b if h else 4 + b)
+                o = 384 * b
+                copy_on("VVSS"[b], T.dn[:, o + p:o + e], buf[:, c:c + e - p], [key], [key, ("dn", o + p, o + e)])
+            if h == 0 and last:
+                act(T.ysb[:, 192:384], T.pa[:, 0:192], Copy, ["bank0"], [("ysb", 192, 384), "bank0"])
+            elif h == 0:
+                ts(T.f0[:, 192:384], T.pa[:, 0:192], 0.0, None, A.is_gt, None, ["bank0"], [("f0", 192, 384), "bank0"])
+        for t in (0, 2, 1, 3):
+            copy_on("VVSS"[t], T.vf[:, t:768:4], T.dn[:, 384 * t:384 * t + 384].indirect(T[nw][:, 0:12]),
+                    [("dn", 384 * t, 384 * t + 384), nw], [("vf", t, 768, 4)])
+        quant("qvf", "svf", "vf", 0, 192)
+        for b in range(4):
+            mm(4 + b, 192, "wq", "wp", 128 * b, "qvf", "svf", 0)
+        renew(4, 0)
+    mm(0, 192, "qvt", "svt", 0, "qx", "sx", 0)
+    op("Y", lambda e: e.dma_start(T.oc[:, 0:768], T.qx[:, 0:192].bitcast(dt.uint8)), [("qx", 0, 192)], [], dma=True)
+    for k in range(4):
+        op("SYSY"[k], lambda e: e.dma_start(T.osc[4 * k:4 * k + 4, :], T.sx[32 * k:32 * k + 4, 0:384]), [("qx", 0, 384)], [], dma=True)
+    cp(T.ysb[:, 0:192], T.pa[:, 0:192], ["bank0"], [("ysb", 0, 192), "bank0"])
+    op("S", lambda e: e.dma_start(T.y[:, :], T.ysb[:, :]), [("ysb", 0, 384)], [], dma=True)
+    wait("G", sorted(total.items()))

@@ -5,29 +5,30 @@ C, H, N = 384, 192, 8
 ROUNDS = 3
 STEPS = [4, 1, 2]
 PARTS = ((0, 256), (256, 384))
+MV = 800
 
 SCRATCH = {
     "xt": ("sbuf", [128, 1536], "bfloat16"), "yb": ("sbuf", [128, 1536], "bfloat16"),
     "xh": ("sbuf", [128, 1536], "bfloat16"), "xg": ("sbuf", [128, 1536], "bfloat16"),
     "qx": ("sbuf", [128, 384], "float8_e4m3fn_x4"), "sx": ("sbuf", [128, 384], "uint8"),
-    "ua": ("sbuf", [128, 520], "bfloat16"), "ub": ("sbuf", [128, 512], "bfloat16"), "vt": ("sbuf", [128, 512], "bfloat16"),
-    "qua": ("sbuf", [128, 130], "float8_e4m3fn_x4"), "sua": ("sbuf", [128, 130], "uint8"),
+    "ua": ("sbuf", [128, 512], "bfloat16"), "vt": ("sbuf", [128, 512], "bfloat16"),
+    "qua": ("sbuf", [128, 128], "float8_e4m3fn_x4"), "sua": ("sbuf", [128, 128], "uint8"),
     "qub": ("sbuf", [128, 128], "float8_e4m3fn_x4"), "sub": ("sbuf", [128, 128], "uint8"),
     "qvt": ("sbuf", [128, 128], "float8_e4m3fn_x4"), "svt": ("sbuf", [128, 128], "uint8"),
     "wq": ("sbuf", [128, 512], "float8_e4m3fn_x4"), "wp": ("sbuf", [128, 512], "uint8"),
-    "nlb": ("sbuf", [128, 48], "int32"), "nla": ("sbuf", [128, 192], "int32"), "pn": ("sbuf", [128, 48], "uint16"),
-    "kk": ("sbuf", [128, 144], "int32"), "clu": ("sbuf", [128, 6], "uint16"), "oe": ("sbuf", [128, 32], "uint16"),
+    "nlb": ("sbuf", [128, 24], "int32"), "nla": ("sbuf", [128, 96], "int32"), "pn": ("sbuf", [128, 24], "uint16"),
+    "kk": ("sbuf", [128, 96], "int32"), "kf": ("sbuf", [128, 8], "float32"), "clu": ("sbuf", [128, 16], "uint16"),
+    "ul": ("sbuf", [128, 8], "uint16"),
     "ci": ("sbuf", [128, 384], "bfloat16"), "nmt": ("sbuf", [128, 384], "float32"),
-    "one": ("sbuf", [128, 2048], "bfloat16"), "et": ("sbuf", [128, 2048], "bfloat16"),
+    "one": ("sbuf", [128, 512], "bfloat16"), "et": ("sbuf", [128, 2048], "bfloat16"),
     "qe": ("sbuf", [128, 512], "float8_e4m3fn_x4"), "se": ("sbuf", [128, 512], "uint8"),
-    "f0": ("sbuf", [128, 384], "bfloat16"), "f1": ("sbuf", [128, 384], "bfloat16"), "f2": ("sbuf", [128, 384], "bfloat16"),
-    "sg1": ("sbuf", [128, 384], "bfloat16"), "sg2": ("sbuf", [128, 384], "bfloat16"),
-    "li0": ("sbuf", [128, 400], "bfloat16"), "li1": ("sbuf", [128, 400], "bfloat16"),
+    "sg": ("sbuf", [128, 192], "bfloat16"),
+    "fl": ("sbuf", [128, 384], "bfloat16"), "li": ("sbuf", [128, 416], "bfloat16"), "lin": ("sbuf", [128, 384], "bfloat16"),
     "pp": ("sbuf", [128, 384], "float32"), "dl": ("sbuf", [128, 384], "float32"),
-    "tt": ("sbuf", [128, 1536], "bfloat16"), "td": ("sbuf", [128, 192], "float32"), "dd": ("sbuf", [128, 192], "float32"),
-    "zn": ("sbuf", [128, 1536], "bfloat16"), "nu": ("sbuf", [128, 400], "bfloat16"), "nmu": ("sbuf", [128, 384], "float32"),
-    "tn": ("sbuf", [128, 768], "bfloat16"), "te": ("sbuf", [128, 768], "bfloat16"),
-    "bw": ("sbuf", [128, 384], "bfloat16"), "eu": ("sbuf", [128, 400], "bfloat16"), "ew": ("sbuf", [128, 64], "uint16"),
+    "tt": ("sbuf", [128, 1600], "bfloat16"), "td": ("sbuf", [128, 192], "float32"), "dd": ("sbuf", [128, 192], "float32"),
+    "zn": ("sbuf", [128, 1536], "bfloat16"), "nu": ("sbuf", [128, 416], "bfloat16"), "nmu": ("sbuf", [128, 384], "float32"),
+    "tn": ("sbuf", [128, 800], "bfloat16"), "te": ("sbuf", [128, 800], "bfloat16"),
+    "bw": ("sbuf", [128, 384], "bfloat16"), "eu": ("sbuf", [128, 224], "bfloat16"), "ew": ("sbuf", [128, 64], "uint16"),
     "dn": ("sbuf", [128, 1536], "bfloat16"), "vo": ("sbuf", [128, 768], "bfloat16"), "vf": ("sbuf", [128, 768], "bfloat16"),
     "qvo": ("sbuf", [128, 192], "float8_e4m3fn_x4"), "svo": ("sbuf", [128, 192], "uint8"),
     "qvf": ("sbuf", [128, 192], "float8_e4m3fn_x4"), "svf": ("sbuf", [128, 192], "uint8"),
@@ -36,16 +37,24 @@ SCRATCH = {
 }
 for _r in range(ROUNDS):
     SCRATCH["nw%d" % _r] = ("sbuf", [128, 32], "uint16")
+    SCRATCH["ns%d" % _r] = ("sbuf", [128, 32], "uint16")
+    SCRATCH["st%d" % _r] = ("sbuf", [128, 64], "uint16")
+    SCRATCH["fin%d" % _r] = ("sbuf", [128, 48], "uint16")
     SCRATCH["ip%d" % _r] = ("sbuf", [128, 24], "uint16")
     SCRATCH["qz%d" % _r] = ("sbuf", [128, 384], "float8_e4m3fn_x4")
     SCRATCH["sz%d" % _r] = ("sbuf", [128, 384], "uint8")
     SCRATCH["lq%d" % _r] = ("sbuf", [128, 384], "float8_e4m3fn_x4")
     SCRATCH["lz%d" % _r] = ("sbuf", [128, 384], "uint8")
-for _r in range(3 * ROUNDS + 1):
-    SCRATCH["iw%d" % _r] = ("sbuf", [128, 64], "uint16")
+for _r in range(3):
+    SCRATCH["ow%d" % _r] = ("sbuf", [128, 32], "uint16")
+    SCRATCH["nx%d" % _r] = ("sbuf", [128, 32], "uint16")
 
 SEMAPHORES = ["cV", "cS", "cP", "cG", "sent"] + ["d%d" % k for k in range(24)] \
     + ["al%d" % k for k in range(ROUNDS)] + ["az%d" % k for k in range(2 * ROUNDS)]
+
+AFTER = ("z0", "z1", "n", "nwrap", "bw", "eu", "unpack0:VVSS", "ewrap", "vo:SVSV", "unpack1:SVSS", "own", "vf:VSSS",
+         "renew_own:VSSS", "far", "ahead", "codes_own", "renew_far:SSSV", "score_own:S", "codes_far", "diffs", "nmove",
+         "score_far:V", "names")
 
 
 def rank_program(g, core, T, topo):
@@ -120,6 +129,14 @@ def rank_program(g, core, T, topo):
     def bank(j):
         return (T.pa if j < 4 else T.pb), 512 * (j % 4), "bank%d" % j
 
+    spare, held = list(range(8)), {}
+
+    def take(n):
+        js = spare[:n]
+        del spare[:n]
+        assert len(js) == n
+        return js
+
     def mm(j, n, lq, ls, la, rq, rs, ra):
         buf, o, key = bank(j)
         op("P", lambda e: e.matmul_mx(buf[:, o:o + n], T[lq][:, la:la + 128], T[ls][:, la:la + 128],
@@ -142,265 +159,328 @@ def rank_program(g, core, T, topo):
     def cp(out, a, reads, writes):
         op("V", lambda e: e.tensor_copy(out, a), reads, writes)
 
-    def act(out, a, fn, reads, writes, scale=1.0):
-        op("S", lambda e: e.activation(out, a, fn, scale=scale), reads, writes)
+    def act(out, a, reads, writes, scale=1.0):
+        if scale == 1.0:
+            op("S", lambda e: e.activation(out, a, Copy), reads, writes)
+        else:
+            op("S", lambda e: e.activation(out, a, Copy, scale=scale), reads, writes)
 
     def copy_on(q, out, a, reads, writes):
         if q == "V":
             cp(out, a, reads, writes)
         else:
-            act(out, a, Copy, reads, writes)
+            act(out, a, reads, writes)
 
     def load(q, out, src, key):
         op(q, lambda e: e.dma_start(out, src), [], [key], dma=True)
 
-    def iota(buf, pattern, base, key, cm=0, a=None):
-        out = T[buf][:, :] if a is None else T[buf][:, a[0]:a[1]]
-        if buf == "kk":
-            op("G", lambda e: e.iota(out, pattern, base, cm), [], [key])
+    def iota(out, pattern, base, keys, cm=0, whole=False):
+        if whole:
+            op("G", lambda e: e.iota(out, pattern, base, cm), [], keys)
         else:
-            op("G", lambda e: e.iota(out, pattern, base, cm, allow_small_or_imprecise_dtypes=True), [], [key])
+            op("G", lambda e: e.iota(out, pattern, base, cm, allow_small_or_imprecise_dtypes=True), [], keys)
 
-    shifted = ["tsh%d" % a for a in range(4)]
-    load("Y", T.nlb[0:112, 24:48], T.nl[16:128, :], "nlb.a")
-    load("S", T.nlb[112:128, 24:48], T.nl[0:16, :], "nlb.b")
-    load("Y", T.nlb[:, 0:24], T.nl[:, :], "nlb.c")
+    def fill(out, keys):
+        op("V", lambda e: e.memset(out, 0.0), [], keys)
+
+    moved = ["mv%d" % a for a in range(4)]
+    load("Y", T.nlb[48:128, :], T.nl[0:80, :], "nlb.a")
+    load("S", T.nlb[0:48, :], T.nl[80:128, :], "nlb.b")
+    load("Y", T.ua[:, :], T.u[:, :], ("ua", 0, 512))
     load("S", T.xt[:, :], T.x[:, :], ("xt", 0, 1536))
-    load("Y", T.ua[:, 0:512], T.u[:, :], ("ua", 0, 512))
-    load("Y", T.ua[:, 512:520], T.u[:, 0:8], ("ua", 512, 520))
-    load("Y", T.ub[:, 0:508], T.u[:, 4:512], ("ub", 0, 508))
-    load("Y", T.ub[:, 508:512], T.u[:, 0:4], ("ub", 508, 512))
     load("Y", T.wq[:, :].bitcast(dt.uint8), T.wc[:, :], ("wq", 0, 512))
     load("Y", T.wp[:, :], T.ws[:, :], ("wp", 0, 512))
     load("Y", T.vt[:, :], T.v[:, :], ("vt", 0, 512))
 
-    iota("kk", [[0, 6]], 0, ("kk", 0, 6), 1, (0, 6))
-    iota("kk", [[16, 6]], 0, ("kk", 6, 12), 0, (6, 12))
-    iota("ci", [[1, 384]], -192, "ci")
-    op("G", lambda e: e.iota(T.tt[:, :], [[0, 1536]], 0, 0, allow_small_or_imprecise_dtypes=True), [], ["tt"] + shifted)
-    iota("tn", [[0, 768]], 0, "tn")
-    iota("te", [[0, 768]], 0, "te")
-    iota("eu", [[0, 400]], 0, "eu")
-    iota("one", [[0, 2048]], 1, "one")
-    op("G", lambda e: e.affine_select(T.et[:, :], T.one[:, :], [[-1, 4], [1, 512]], A.is_equal, 0.0, 0, -4), ["one"], ["et"])
-    op("V", lambda e: e.memset(T.td[:, :], 0.0), [], ["td"])
-
-    def kc(i):
-        return T.kk[:, 6 * i:6 * i + 6]
+    def kc(i, n=3):
+        return T.kk[:, 8 * i:8 * i + n]
 
     def kr(*i):
-        return [("kk", 6 * j, 6 * j + 6) for j in i]
-    ts(kc(2), kc(0), 15, None, A.bitwise_and, None, kr(0), kr(2))
-    ts(kc(3), kc(0), 4, 1, A.logical_shift_right, A.bitwise_and, kr(0), kr(3))
-    tt(kc(4), kc(2), kc(1), A.add, kr(2, 1), kr(4))
-    ts(kc(17), kc(3), -784, 768, A.mult, A.add, kr(3), kr(17))
-    ts(kc(5), kc(4), 31, None, A.bitwise_and, None, kr(4), kr(5))
-    ts(kc(18), kc(4), 32, None, A.is_lt, None, kr(4), kr(18))
-    ts(kc(20), kc(4), 64, 12, A.is_ge, A.mult, kr(4), kr(20))
-    ts(kc(21), kc(4), 64, None, A.is_ge, None, kr(4), kr(21))
-    tt(kc(22), kc(5), kc(20), A.add, kr(5, 20), kr(22))
-    tt(kc(23), kc(18), kc(21), A.add, kr(18, 21), kr(23))
-    ts(kc(6), kc(22), 24, -24, A.is_ge, A.mult, kr(22), kr(6))
-    tt(kc(19), kc(17), kc(23), A.mult, kr(17, 23), kr(19))
-    tt(kc(7), kc(22), kc(6), A.add, kr(22, 6), kr(7))
-    tt(kc(8), kc(7), kc(3), A.add, kr(7, 3), kr(8))
-    ts(kc(10), kc(7), 0, 384, A.is_equal, A.mult, kr(7), kr(10))
-    ts(kc(12), kc(7), 16, None, A.mult, None, kr(7), kr(12))
-    ts(kc(9), kc(8), 1, None, A.bitwise_and, None, kr(8), kr(9))
-    tt(kc(11), kc(10), kc(3), A.mult, kr(10, 3), kr(11))
-    ts(kc(13), kc(9), 368, None, A.mult, None, kr(9), kr(13))
-    tt(kc(14), kc(11), kc(19), A.add, kr(11, 19), kr(14))
-    tt(kc(15), kc(12), kc(13), A.add, kr(12, 13), kr(15))
-    tt(kc(16), kc(14), kc(15), A.add, kr(14, 15), kr(16))
-    cp(T.clu[:, :], kc(16), kr(16), ["clu"])
+        return [("kk", 8 * j, 8 * j + 8) for j in i]
 
-    nl = ["nlb.a", "nlb.b", "nlb.c"]
-    ts(T.nla[:, 0:48], T.nlb[:, :], 1, None, A.bitwise_and, None, nl, [("nla", 0, 48)])
-    ts(T.nla[:, 48:96], T.nlb[:, :], 1, None, A.logical_shift_right, None, nl, [("nla", 48, 96)])
-    ts(T.nla[:, 96:144], T.nla[:, 0:48], 192, None, A.mult, None, [("nla", 0, 48)], [("nla", 96, 144)])
-    tt(T.nla[:, 144:192], T.nla[:, 48:96], T.nla[:, 96:144], A.add, [("nla", 48, 144)], [("nla", 144, 192)])
-    cp(T.pn[:, :], T.nla[:, 144:192], [("nla", 144, 192)], ["pn"])
-    cp(T.li0[:, 0:384].indirect(T.pn[:, 24:48]), T.ci[:, :], ["pn", "ci"], [("li0", 0, 384)])
-    cp(T.li0[:, 384:400], T.li0[:, 0:16], [("li0", 0, 16)], [("li0", 384, 400)])
-    quant("qua", "sua", "ua", 0, 130)
+    def col(i):
+        return T.kf[:, i:i + 1]
+    iota(kc(0, 1), [[0, 1]], 0, kr(0), 1, True)
+    iota(kc(1), [[16, 3]], 0, kr(1), 0, True)
+    iota(kc(2, 8), [[16, 8]], 80, kr(2), 0, True)
+    iota(T.ci[:, :], [[1, 384]], -192, ["ci"])
+    iota(T.tt[:, MV:2 * MV], [[0, MV]], 0, moved)
+    iota(T.te[:, :], [[0, 800]], 0, ["te"])
+    iota(T.one[:, :], [[0, 512]], 1, ["one"])
+    for b in range(4):
+        op("G", lambda e: e.affine_select(T.et[:, 512 * b:512 * b + 512], T.one[:, :], [[1, 512]], A.is_equal, 0.0, -b, -4),
+           ["one"], [("et", 512 * b, 512 * b + 512)])
+    iota(T.nmt[:, :], [[1, 2], [2, 192]], 0, ["nmt"])
+    fill(T.td[:, :], ["td"])
+    for buf, end in (("li", 400), ("nu", 400), ("eu", 208)):
+        fill(T[buf][:, 0:16], [(buf, 0, 16)])
+        fill(T[buf][:, end:end + 16], [(buf, end, end + 16)])
+
+    def const(c, n, add, by=None):
+        if by is None:
+            ts(T.clu[:, c:c + n], kc(10, n), add, None, A.add, None, kr(10), [("clu", c, c + n)])
+        else:
+            ts(T.clu[:, c:c + n], kc(10, n), col(by), add, A.add, A.add, kr(10) + [("kf", by, by + 1)], [("clu", c, c + n)])
+    ts(kc(3, 1), kc(0, 1), 15, None, A.bitwise_and, None, kr(0), kr(3))
+    ts(kc(4, 1), kc(0, 1), 4, None, A.logical_shift_right, None, kr(0), kr(4))
+    cp(col(0), kc(3, 1), kr(3), [("kf", 0, 1)])
+    tt(kc(5, 1), kc(0, 1), kc(4, 1), A.add, kr(0, 4), kr(5))
+    ts(kc(6, 1), kc(4, 1), 1, None, A.bitwise_and, None, kr(4), kr(6))
+    ts(kc(7), kc(1), col(0), None, A.add, None, kr(1) + [("kf", 0, 1)], kr(7))
+    ts(kc(5, 1), kc(5, 1), 1, None, A.bitwise_and, None, kr(5), kr(5))
+    ts(col(1), kc(3, 1), 17.0, None, A.mult, None, kr(3), [("kf", 1, 2)])
+    ts(kc(8), kc(7), 24.0, -24.0, A.is_ge, A.mult, kr(7), kr(8))
+    ts(col(2), kc(5, 1), 400.0, None, A.mult, None, kr(5), [("kf", 2, 3)])
+    ts(kc(11, 8), kc(2, 8), col(1), None, A.add, None, kr(2) + [("kf", 1, 2)], kr(11))
+    tt(kc(9), kc(7), kc(8), A.add, kr(7, 8), kr(9))
+    ts(col(3), kc(6, 1), 768.0, 16.0, A.mult, A.add, kr(6), [("kf", 3, 4)])
+    ts(kc(11, 8), kc(11, 8), 127, None, A.bitwise_and, None, kr(11), kr(11))
+    ts(kc(10), kc(9), 16.0, col(2), A.mult, A.add, kr(9) + [("kf", 2, 3)], kr(10))
+    ts(col(4), kc(6, 1), -17.0, 3.0, A.mult, A.add, kr(6), [("kf", 4, 5)])
+    cp(T.ul[:, :], kc(11, 8), kr(11), ["ul"])
+    OWN, NEXT, SRC, NSRC = (0, 4, 10), (2, 6), 8, 14
+    const(OWN[0], 2, 0.0)
+    const(NEXT[0], 2, 0.0, 3)
+
+    nl = ["nlb.a", "nlb.b"]
+    ts(T.nla[:, 0:24], T.nlb[:, :], 1, None, A.bitwise_and, None, nl, [("nla", 0, 24)])
+    ts(T.nla[:, 24:48], T.nlb[:, :], 1, None, A.logical_shift_right, None, nl, [("nla", 24, 48)])
+    ts(T.nla[:, 48:72], T.nla[:, 0:24], 192, None, A.mult, None, [("nla", 0, 24)], [("nla", 48, 72)])
+    const(OWN[1], 2, 1.0)
+    tt(T.nla[:, 72:96], T.nla[:, 24:48], T.nla[:, 48:72], A.add, [("nla", 24, 72)], [("nla", 72, 96)])
+    const(NEXT[1], 2, 1.0, 3)
+    cp(T.pn[:, :], T.nla[:, 72:96], [("nla", 72, 96)], ["pn"])
+    quant("qua", "sua", "ua", 0, 128)
+    cp(T.li[:, 16:400].indirect(T.pn[:, :]), T.ci[:, :], ["pn", "ci"], [("li", 16, 400)])
+    cp(T.qub[:, :].bitcast(dt.uint32), T.qua[:, :].bitcast(dt.uint32).indirect(T.ul[:, :]), ["qua", "ul"], ["qub"])
+    act(T.sub[:, :], T.sua[:, :].indirect(T.ul[:, :]), ["qua", "ul"], ["sub"])
     quant("qx", "sx", "xt", 0, 384)
+    mm(0, 384, "qub", "sub", 0, "qx", "sx", 0)
 
-    def transposes(dst, src, parts):
-        for o, a, n in parts:
-            op("V", lambda e: e.transpose(T[dst][:, o:o + n], T[src][:, a:a + n]), [(src, a, a + n)], [(dst, o, o + n)])
+    def transposes(dst, src, n=384):
+        op("V", lambda e: e.transpose(T[dst][:, 0:n], T[src][:, 16:16 + n]), [(src, 16, 16 + n)], [(dst, 0, n)])
+        op("V", lambda e: e.transpose(T[dst][:, 384:416 + n], T[src][:, 0:n + 32]), [(src, 0, n + 32)], [(dst, 384, 416 + n)])
 
-    def move():
-        for a in range(4):
-            b = (a + 1) % 4
-            cp(T.tt[32 * b:32 * b + 32, 768:1536:32], T.tt[32 * a:32 * a + 32, 16:768:32], [("tt", 0, 768)], ["tsh%d" % b])
+    def move(src, row, step, to, by):
+        n = 64 if by == 2 else 32
+        for a in range(0, 128, n):
+            b = (a + 32 * by) % 128
+            act(T.tt[b:b + n, MV + to:2 * MV:step], T[src][a:a + n, row:MV:step], [(src, 0, MV)],
+                [("mv%d" % k, to, MV, step) for k in range(b // 32, (b + n) // 32)])
 
-    def tables(k):
-        ts(T["iw%d" % k][:, 0:64], T.tt[:, 0:1536].indirect(T.clu[:, 0:4]), 192.0, None, A.add, None,
-           [("tt", 0, 768), "clu"] + shifted, ["iw%d" % k])
+    def table(out, src, a, b, c, n, extra=()):
+        ts(T[out][:, 0:16 * n], T[src][:, a:b].indirect(T.clu[:, c:c + n]), 192.0, None, A.add, None,
+           [("clu", c, c + n)] + ([(src, 0, MV)] if a == 0 else []) + (moved if b > MV else []), [out])
 
-    def diff_same():
-        tt(T.td[:, 16:192:32], T.tt[:, 192:384:32], T.tt[:, 0:192:32], A.subtract, [("tt", 0, 384)], [("td", 16, 192, 32)])
-
-    def diff_next():
-        tt(T.td[:, 0:192:32], T.tt[:, 960:1152:32], T.tt[:, 768:960:32], A.subtract, shifted, [("td", 0, 192, 32)])
+    def diff(to, step, a, b, reads):
+        tt(T.td[:, to:192:step], T.tt[:, a + 192:a + 384:step], T.tt[:, a:a + 192:step], A.subtract, reads, [("td", to, 192, step)])
 
     def diff_back():
         op("V", lambda e: e.transpose(T.dd[:, :], T.td[:, :]), [("td", 0, 192)], ["dd"])
 
-    def wrap(src, k, diffs):
-        transposes("tt", src, [(0, 0, 384), (384, 16, 384)])
-        if diffs:
-            diff_same()
-        move()
-        if diffs:
-            diff_next()
-            tables(k)
-            diff_back()
-        else:
-            ts(T.oe[:, :], T.tt[:, 0:1536].indirect(T.clu[:, 4:6]), 192.0, None, A.add, None,
-               [("tt", 0, 768), "clu"] + shifted, ["oe"])
+    def wrap(k, row, to):
+        transposes("tt", "li")
+        move("tt", row, 32, row, 3)
+        tt(T.td[:, to:192:16], T.tt[:, row + 192:384:16], T.tt[:, row:192:16], A.subtract, [("tt", 0, 384)], [("td", to, 192, 16)])
+        table("ow%d" % k, "tt", 0, MV, OWN[row], 2)
+        diff_back()
+
+    def unwrap(lst, a):
+        act(T.lin[:, :], T.ci[:, :].indirect(T[lst][:, a:a + 24]), ["ci", lst], ["lin"])
 
     def send(dst, out, src, sem):
         rid, pid = topo.addr(dst, core)
         g.remote_dma(out, src, T.sem[sem], T.sem.sent, pid, rid, topo.mask(core, dst))
         total["sent"] = total.get("sent", 0) + len(topo.engines(core, dst))
 
-    wrap("li0", 0, True)
-    cur, li = 0, 0
+    wrap(0, 0, 0)
+    ts(T.fl[:, :], T.pa[:, 0:384], 0.0, None, A.is_gt, None, ["bank0"], [("fl", 0, 384), "bank0"])
+    table("nx0", "tt", 0, 2 * MV, NEXT[0], 2)
+    unwrap("nx0", 0)
     for r in range(ROUNDS):
         last = r == ROUNDS - 1
         to, frm = T.cores[(rank + STEPS[r]) % N], T.cores[(rank - STEPS[r]) % N]
         nin = len(topo.engines(frm, core))
-        own = "pn" if r == 0 else "nw%d" % (r - 1)
-        nw, qz, sz, lq, lz, ip = ("%s%d" % (k, r) for k in ("nw", "qz", "sz", "lq", "lz", "ip"))
-        n = 384 if r == 0 else 192
-        mm(0, n, "qua", "sua", 0, "qx", "sx", 0)
-        ts(T.f0[:, 0:n], T.pa[:, 0:n], 0.0, None, A.is_gt, None, ["bank0"], [("f0", 0, n), "bank0"])
-        if r == 0:
-            quant("qub", "sub", "ub", 0, 128)
-        mm(1, 384, "qub", "sub", 0, "qx", "sx", 0)
-        mm(2, 384, "qua", "sua", 2, "qx", "sx", 0)
+        nw, qz, sz, lq, lz, ip, fin, st, ns = ("%s%d" % (k, r) for k in ("nw", "qz", "sz", "lq", "lz", "ip", "fin", "st", "ns"))
 
         def beside(j):
-            if j == 0:
-                for k in (1, 2):
-                    act(T["sg%d" % k][:, :], T.pa[:, 512 * k:512 * k + 384], Sign, ["bank%d" % k], ["sg%d" % k, "bank%d" % k])
-                    act(T["f%d" % k][:, :], T["sg%d" % k][:, :], Relu, ["sg%d" % k], ["f%d" % k])
-            for t in ((0, 1), (2, 3), ())[j]:
-                act(T.xh[:, 384 * t:384 * t + 384], T.xt[:, t:1536:4], Copy, [("xt", t, 1536, 4)],
+            for t in ((0,), (1, 2), (3,))[j]:
+                act(T.xh[:, 384 * t:384 * t + 384], T.xt[:, t:1536:4], [("xt", t, 1536, 4)],
                     [("xh", 384 * t, 384 * t + 384)], scale=0.5)
-            if j == 1:
-                for t in range(4):
-                    for h in range(2):
-                        o = 384 * t + 192 * h
-                        act(T.xg[:, o:o + 192], T.xt[:, 4 * h + t:1536:8], Copy, [("xt", 4 * h + t, 1536, 8)],
-                            [("xg", o, o + 192)], scale=0.5)
-            if j == 2 and r == 0:
-                act(T.yb[:, :], T.xt[:, :], Copy, [("xt", 0, 1536)], [("yb", 0, 1536)], scale=32.0)
+            for t in ((0,), (1,), (2, 3))[j]:
+                for h in range(2):
+                    o = 384 * t + 192 * h
+                    act(T.xg[:, o:o + 192], T.xt[:, 4 * h + t:1536:8], [("xt", 4 * h + t, 1536, 8)],
+                        [("xg", o, o + 192)], scale=0.5)
+            if j == 1 and r == 0:
+                act(T.yb[:, :], T.xt[:, :], [("xt", 0, 1536)], [("yb", 0, 1536)], scale=32.0)
         for j in range(3):
-            iw, f, lo, ln = "iw%d" % cur, "f%d" % j, "li%d" % li, "li%d" % (1 - li)
-            tt(T.pp[:, 0:192], T[f][:, 0:384].indirect(T[iw][:, 0:12]), T.dd[:, :], A.mult, [f, iw, "dd"], [("pp", 0, 192)])
-            if j == 0:
-                ts(T.pp[:, 192:384], T.pp[:, 0:192], -1.0, None, A.mult, None, [("pp", 0, 192)], [("pp", 192, 384)])
-                act(T.dl[:, 192:384], T.pp[:, 0:384].indirect(T[own][:, 12:24]), Copy, [("pp", 0, 384), own], [("dl", 192, 384)])
-                cp(T.dl[:, 0:192], T.pp[:, 0:384].indirect(T[own][:, 0:12]), [("pp", 0, 384), own], [("dl", 0, 192)])
+            if j == 0 and r > 0:
+                iw, nx, na, own = "st%d" % (r - 1), "st%d" % (r - 1), 32, "ns%d" % (r - 1)
             else:
-                act(T.pp[:, 192:384], T.pp[:, 0:192], Copy, [("pp", 0, 192)], [("pp", 192, 384)], scale=-1.0)
+                iw, nx, na, own = "ow%d" % j, "nx%d" % j, 0, "pn"
+            tt(T.pp[:, 0:192], T.fl[:, 0:384].indirect(T[iw][:, 0:12]), T.dd[:, :], A.mult, ["fl", iw, "dd"], [("pp", 0, 192)])
+            if j == 0:
+                if r == 0:
+                    const(SRC, 2, 0.0, 4)
+                ts(T.pp[:, 192:384], T.pp[:, 0:192], -1.0, None, A.mult, None, [("pp", 0, 192)], [("pp", 192, 384)])
+                if r == 0:
+                    const(OWN[2], 3, 2.0)
+                act(T.dl[:, 192:384], T.pp[:, 0:384].indirect(T[own][:, 12:24]), [("pp", 0, 384), own], [("dl", 192, 384)])
+                cp(T.dl[:, 0:192], T.pp[:, 0:384].indirect(T[own][:, 0:12]), [("pp", 0, 384), own], [("dl", 0, 192)])
+                if r == 0:
+                    const(NSRC, 2, 2.0, 4)
+            else:
+                table(nx, "tt", 0, 2 * MV, NEXT[j - 1], 2)
+                act(T.pp[:, 192:384], T.pp[:, 0:192], [("pp", 0, 192)], [("pp", 192, 384)], scale=-1.0)
+                unwrap(nx, 0)
                 for h in range(2):
                     cp(T.dl[:, 0:384].indirect(T[iw][:, 12 * h:12 * h + 12]), T.pp[:, 192 * h:192 * h + 192],
                        [("pp", 192 * h, 192 * h + 192), iw], ["dl"])
-            tt(T[ln][:, 0:400], T.dl[:, 0:384].indirect(T[iw][:, 32:57]), T[lo][:, 0:400], A.add,
-               ["dl", iw, (lo, 0, 400)], [(ln, 0, 400)])
+            tt(T.li[:, 16:400], T.dl[:, 0:384].indirect(T[nx][:, na:na + 24]), T.lin[:, :], A.add,
+               ["dl", nx, "lin"], [("li", 16, 400)])
             beside(j)
-            li, cur = 1 - li, cur + 1
-            wrap(ln, cur, j < 2)
-        iw = "iw%d" % cur
-        for h, (a, b) in enumerate(PARTS):
+            if j < 2:
+                wrap(j + 1, j, j + 1)
+        transposes("tt", "li")
+        table(fin, "tt", 0, MV, OWN[2], 3)
+        wait("G", [("cV", total["cV"])])
+        send(to, T[ip][:, 0:24], T[fin][:, 0:24], "al%d" % r)
+        note(("al%d" % r, nin), [], [ip])
+        total["al%d" % r] = nin
+        if not last:
+            move("tt", 2, 16, 2, 1)
+            move("tt", 18, 32, 3, 2)
+
+        def z(h, _):
+            a, b = PARTS[h]
             az = "az%d" % (2 * r + h)
             for t in range(4):
-                tt(T.zn[:, 4 * a + t:4 * b:4], T.xh[:, 384 * t:384 * t + 384].indirect(T.oe[:, a // 16:b // 16]),
-                   T.xg[:, 384 * t + a:384 * t + b], A.add, [("xh", 384 * t, 384 * t + 384), ("xg", 384 * t, 384 * t + 384), "oe"],
+                tt(T.zn[:, 4 * a + t:4 * b:4], T.xh[:, 384 * t:384 * t + 384].indirect(T[fin][:, 12 + a // 16:12 + b // 16]),
+                   T.xg[:, 384 * t + a:384 * t + b], A.add, [("xh", 384 * t, 384 * t + 384), ("xg", 384 * t, 384 * t + 384), fin],
                    [("zn", 4 * a + t, 4 * b, 4)])
-                if h == 0 and t == 0:
-                    tables(cur)
-                    wait("G", [acc[iw][0][0]])
-                    send(to, T[ip][:, 0:24], T[iw][:, 0:24], "al%d" % r)
-                    note(("al%d" % r, nin), [], [ip])
-                    total["al%d" % r] = nin
             quant(qz, sz, "zn", a, b - a, 4 * a)
             wait("G", [("cV", total["cV"])])
             send(to, T[lq][:, a:b].bitcast(dt.uint8), T[qz][:, a:b].bitcast(dt.uint8), az)
             send(to, T[lz][:, a:b], T[sz][:, a:b], az)
             total[az] = 2 * nin
             note((az, 2 * nin), [], [(lq, a, b)])
-        if r == 0:
-            iota("nmt", [[1, 2], [2, 192]], 0, "nmt")
-        cp(T.nu[:, 0:384].indirect(T[iw][:, 0:24]), T.ci[:, :], [iw, "ci"], [("nu", 0, 384)])
-        cp(T.nu[:, 384:400], T.nu[:, 0:16], [("nu", 0, 16)], [("nu", 384, 400)])
-        transposes("tn", "nu", [(0, 0, 384), (384, 16, 384)])
-        ts(T[nw][:, 0:32], T.tn[:, 0:768].indirect(T.clu[:, 2:4]), 192.0, None, A.add, None, ["tn", "clu"], [nw])
-        act(T.bw[:, :], T.nu[:, 0:384].indirect(T[ip][:, 0:24]), Copy, [("nu", 0, 384), ip], ["bw"])
-        act(T.eu[:, 0:192], T.bw[:, 0:384].indirect(T[nw][:, 12:24]), Copy, ["bw", nw], [("eu", 0, 192)])
-        act(T.eu[:, 384:400], T.eu[:, 0:16], Copy, [("eu", 0, 16)], [("eu", 384, 400)])
-        if not last:
-            diff_same()
-            diff_next()
-            diff_back()
-        else:
-            cp(T.nmu[:, 0:384].indirect(T[iw][:, 0:24]), T.nmt[:, :], [iw, "nmt"], ["nmu"])
-            op("Y", lambda e: e.dma_start(T.nm[:, :], T.nmu[0:128:16, :]), ["nmu"], [], dma=True)
-        if r == 0:
-            quant("qe", "se", "et", 0, 512)
-            quant("qvt", "svt", "vt", 0, 128)
-        transposes("te", "eu", [(0, 0, 192), (384, 16, 192), (736, 368, 32)])
-        for t in (2, 3, 0, 1):
-            ts(T.ew[:, 16 * t:16 * t + 16], T.te[:, 0:768].indirect(T.clu[:, 2:3]), 4.0, 768.0 + t, A.mult, A.add,
-               ["te", "clu"], [("ew", 16 * t, 16 * t + 16)])
-        for t in (2, 0, 3, 1):
-            copy_on("VVSS"[t], T.vo[:, t:768:4], T.zn[:, 0:1536].indirect(T.ew[:, 16 * t:16 * t + 12]),
-                    [("zn", 0, 1536), ("ew", 16 * t, 16 * t + 16)], [("vo", t, 768, 4)])
-        quant("qvo", "svo", "vo", 0, 192)
-        for b in range(4):
-            mm(b, 192, "wq", "wp", 128 * b, "qvo", "svo", 0)
 
-        def renew(first, o):
+        def names_by_column(_):
+            cp(T.nu[:, 16:400].indirect(T[fin][:, 0:24]), T.ci[:, :], [fin, "ci"], [("nu", 16, 400)])
+            if r == 0:
+                quant("qe", "se", "et", 0, 512)
+
+        def nwrap(_):
+            transposes("tn", "nu")
+            table(nw, "tn", 0, MV, OWN[0], 2)
+
+        def bw(_):
+            act(T.bw[:, :], T.nu[:, 16:400].indirect(T[ip][:, 0:24]), [("nu", 16, 400), ip], ["bw"])
+
+        def eu(_):
+            act(T.eu[:, 16:208], T.bw[:, 0:384].indirect(T[nw][:, 12:24]), ["bw", nw], [("eu", 16, 208)])
+
+        def ewrap(_):
+            transposes("te", "eu", 192)
+            for t in range(4):
+                ts(T.ew[:, 16 * t:16 * t + 16], T.te[:, 0:800].indirect(T.clu[:, 0:1]), 4.0, 768.0 + t, A.mult, A.add,
+                   ["te", ("clu", 0, 2)], [("ew", 16 * t, 16 * t + 16)])
+
+        def vo(qs):
+            for t in range(4):
+                copy_on(qs[t], T.vo[:, t:768:4], T.zn[:, 0:1536].indirect(T.ew[:, 16 * t:16 * t + 12]),
+                        [("zn", 0, 1536), ("ew", 16 * t, 16 * t + 16)], [("vo", t, 768, 4)])
+
+        def unpack(h, qs):
+            p, e = PARTS[h]
+            js = take(4)
             for b in range(4):
-                buf, c, key = bank(first + b)
+                mm(js[b], e - p, "qe", "se", 128 * b, lq, lz, p)
+            for b in range(4):
+                buf, c, key = bank(js[b])
+                o = 384 * b
+                copy_on(qs[b], T.dn[:, o + p:o + e], buf[:, c:c + e - p], [key], [key, ("dn", o + p, o + e)])
+            spare.extend(js)
+
+        def vf(qs):
+            for t in range(4):
+                copy_on(qs[t], T.vf[:, t:768:4], T.dn[:, 384 * t:384 * t + 384].indirect(T[nw][:, 0:12]),
+                        [("dn", 384 * t, 384 * t + 384), nw], [("vf", t, 768, 4)])
+
+        def layer(o, q, s, v):
+            quant(q, s, v, 0, 192)
+            held[o] = take(4)
+            for b in range(4):
+                mm(held[o][b], 192, "wq", "wp", 128 * b, q, s, 0)
+
+        def renew(o, qs):
+            for b in range(4):
+                buf, c, key = bank(held[o][b])
                 y = T.yb[:, o + b:o + 768:4]
                 tt(y, buf[:, c:c + 192], y, A.add, [key, ("yb", o + b, o + 768, 4)], [key, ("yb", o + b, o + 768, 4)])
                 k = ([("yb", o + b, o + 768, 4)], [("xt", o + b, o + 768, 4)])
-                if b < 3:
-                    act(T.xt[:, o + b:o + 768:4], y, Copy, *k, scale=2.0 ** -5)
+                if qs[b] == "S":
+                    act(T.xt[:, o + b:o + 768:4], y, *k, scale=2.0 ** -5)
                 else:
                     ts(T.xt[:, o + b:o + 768:4], y, 2.0 ** -5, None, A.mult, None, *k)
+            spare.extend(held[o])
+
+        def codes(o):
             quant("qx", "sx", "xt", o // 4, 192, o)
-        renew(0, 768)
-        if last:
-            op("Y", lambda e: e.dma_start(T.oc[:, 768:1536], T.qx[:, 192:384].bitcast(dt.uint8)), [("qx", 192, 384)], [], dma=True)
-        for h, (p, e) in enumerate(PARTS):
-            for b in (1, 2, 3, 0):
-                mm(b if h else 4 + b, e - p, "qe", "se", 128 * b, lq, lz, p)
-            if h == 0:
-                mm(0, 192, "qvt" if last else "qua", "svt" if last else "sua", 0, "qx", "sx", 192)
-            for b in (1, 2, 3, 0):
-                buf, c, key = bank(b if h else 4 + b)
-                o = 384 * b
-                copy_on("VVSS"[b], T.dn[:, o + p:o + e], buf[:, c:c + e - p], [key], [key, ("dn", o + p, o + e)])
-            if h == 0 and last:
-                act(T.ysb[:, 192:384], T.pa[:, 0:192], Copy, ["bank0"], [("ysb", 192, 384), "bank0"])
-            elif h == 0:
-                ts(T.f0[:, 192:384], T.pa[:, 0:192], 0.0, None, A.is_gt, None, ["bank0"], [("f0", 192, 384), "bank0"])
-        for t in (0, 2, 1, 3):
-            copy_on("VVSS"[t], T.vf[:, t:768:4], T.dn[:, 384 * t:384 * t + 384].indirect(T[nw][:, 0:12]),
-                    [("dn", 384 * t, 384 * t + 384), nw], [("vf", t, 768, 4)])
-        quant("qvf", "svf", "vf", 0, 192)
-        for b in range(4):
-            mm(4 + b, 192, "wq", "wp", 128 * b, "qvf", "svf", 0)
-        renew(4, 0)
-    mm(0, 192, "qvt", "svt", 0, "qx", "sx", 0)
-    op("Y", lambda e: e.dma_start(T.oc[:, 0:768], T.qx[:, 0:192].bitcast(dt.uint8)), [("qx", 0, 192)], [], dma=True)
+            if last:
+                op("Y", lambda e: e.dma_start(T.oc[:, o:o + 768], T.qx[:, o // 4:o // 4 + 192].bitcast(dt.uint8)),
+                   [("qx", o // 4, o // 4 + 192)], [], dma=True)
+
+        def score(a, q):
+            j = take(1)[0]
+            buf, c, key = bank(j)
+            if last:
+                mm(j, 192, "qvt", "svt", 0, "qx", "sx", a)
+                copy_on(q, T.ysb[:, a:a + 192], buf[:, c:c + 192], [key], [("ysb", a, a + 192), key])
+                op("S", lambda e: e.dma_start(T.y[:, a:a + 192], T.ysb[:, a:a + 192]), [("ysb", a, a + 192)], [], dma=True)
+            else:
+                mm(j, 192, "qub", "sub", 0, "qx", "sx", a)
+                if q == "V":
+                    ts(T.fl[:, a:a + 192], buf[:, c:c + 192], 0.0, None, A.is_gt, None, [key], [("fl", a, a + 192), key])
+                else:
+                    op("S", lambda e: e.activation(T.sg[:, :], buf[:, c:c + 192], Sign), [key], ["sg", key])
+                    op("S", lambda e: e.activation(T.fl[:, a:a + 192], T.sg[:, :], Relu), ["sg"], [("fl", a, a + 192)])
+            spare.append(j)
+
+        def ahead(_):
+            if r == 0:
+                quant("qvt", "svt", "vt", 0, 128)
+            if not last:
+                table(st, "tt", MV, 2 * MV, SRC, 4)
+                unwrap(st, 32)
+
+        def diffs(_):
+            if not last:
+                diff(0, 32, MV + 3, 0, moved)
+                diff(16, 32, MV + 2, 0, moved)
+                diff_back()
+
+        def nmove(_):
+            if last:
+                act(T.nmu[:, :], T.nmt[:, :].indirect(T[nw][:, 0:24]), ["nmt", nw], ["nmu"])
+                op("Y", lambda e: e.dma_start(T.nm[:, :], T.nmu[0:128:16, :]), ["nmu"], [], dma=True)
+            else:
+                move("tn", 0, 32, 4, 1)
+                move("tn", 16, 32, 5, 2)
+
+        def names(_):
+            if not last:
+                table(ns, "tt", MV, 2 * MV, NSRC, 2)
+
+        steps = {"z0": lambda q: z(0, q), "z1": lambda q: z(1, q), "n": names_by_column, "nwrap": nwrap, "bw": bw, "eu": eu,
+                 "ewrap": ewrap, "vo": vo, "vf": vf, "unpack0": lambda q: unpack(0, q), "unpack1": lambda q: unpack(1, q),
+                 "far": lambda q: layer(0, "qvf", "svf", "vf"), "own": lambda q: layer(768, "qvo", "svo", "vo"),
+                 "renew_far": lambda q: renew(0, q), "renew_own": lambda q: renew(768, q),
+                 "codes_far": lambda q: codes(0), "codes_own": lambda q: codes(768), "nmove": nmove, "diffs": diffs,
+                 "score_far": lambda q: score(0, q), "score_own": lambda q: score(192, q), "ahead": ahead, "names": names}
+        for s in AFTER:
+            steps[s.split(":")[0]](s.split(":")[-1])
     for k in range(4):
-        op("SYSY"[k], lambda e: e.dma_start(T.osc[4 * k:4 * k + 4, :], T.sx[32 * k:32 * k + 4, 0:384]), [("qx", 0, 384)], [], dma=True)
-    cp(T.ysb[:, 0:192], T.pa[:, 0:192], ["bank0"], [("ysb", 0, 192), "bank0"])
-    op("S", lambda e: e.dma_start(T.y[:, :], T.ysb[:, :]), [("ysb", 0, 384)], [], dma=True)
+        op("YSYS"[k], lambda e: e.dma_start(T.osc[4 * k:4 * k + 4, :], T.sx[32 * k:32 * k + 4, 0:384]), [("qx", 0, 384)], [], dma=True)
     wait("G", sorted(total.items()))

@@ -4,8 +4,7 @@ from concourse.mybir import dt, AluOpType, ActivationFunctionType
 C, H, N = 384, 192, 8
 ROUNDS = 3
 STEPS = [4, 1, 2]
-PARTS = ((0, 256), (256, 384))
-MV = 800
+PARTS = ((0, 128), (128, 256), (256, 384))
 
 SCRATCH = {
     "xt": ("sbuf", [128, 1536], "bfloat16"), "yb": ("sbuf", [128, 1536], "bfloat16"),
@@ -16,29 +15,27 @@ SCRATCH = {
     "qub": ("sbuf", [128, 128], "float8_e4m3fn_x4"), "sub": ("sbuf", [128, 128], "uint8"),
     "qvt": ("sbuf", [128, 128], "float8_e4m3fn_x4"), "svt": ("sbuf", [128, 128], "uint8"),
     "wq": ("sbuf", [128, 512], "float8_e4m3fn_x4"), "wp": ("sbuf", [128, 512], "uint8"),
-    "nlb": ("sbuf", [128, 24], "int32"), "nla": ("sbuf", [128, 96], "int32"), "pn": ("sbuf", [128, 24], "uint16"),
-    "kk": ("sbuf", [128, 96], "int32"), "kf": ("sbuf", [128, 8], "float32"), "clu": ("sbuf", [128, 16], "uint16"),
+    "nlb": ("sbuf", [128, 48], "int32"), "nla": ("sbuf", [128, 192], "int32"), "pn": ("sbuf", [128, 48], "uint16"),
+    "kk": ("sbuf", [128, 96], "int32"), "kf": ("sbuf", [128, 8], "float32"), "clu": ("sbuf", [128, 8], "uint16"),
     "ul": ("sbuf", [128, 8], "uint16"),
     "ci": ("sbuf", [128, 384], "bfloat16"), "nmt": ("sbuf", [128, 384], "float32"),
     "one": ("sbuf", [128, 512], "bfloat16"), "et": ("sbuf", [128, 2048], "bfloat16"),
     "qe": ("sbuf", [128, 512], "float8_e4m3fn_x4"), "se": ("sbuf", [128, 512], "uint8"),
-    "sg": ("sbuf", [128, 192], "bfloat16"),
-    "fl": ("sbuf", [128, 384], "bfloat16"), "li": ("sbuf", [128, 416], "bfloat16"), "lin": ("sbuf", [128, 384], "bfloat16"),
-    "pp": ("sbuf", [128, 384], "float32"), "dl": ("sbuf", [128, 384], "float32"),
-    "tt": ("sbuf", [128, 1600], "bfloat16"), "td": ("sbuf", [128, 192], "float32"), "dd": ("sbuf", [128, 192], "float32"),
-    "zn": ("sbuf", [128, 1536], "bfloat16"), "nu": ("sbuf", [128, 416], "bfloat16"), "nmu": ("sbuf", [128, 384], "float32"),
-    "tn": ("sbuf", [128, 800], "bfloat16"), "te": ("sbuf", [128, 800], "bfloat16"),
+    "sg": ("sbuf", [128, 192], "bfloat16"), "fl": ("sbuf", [128, 384], "bfloat16"), "pp": ("sbuf", [128, 384], "float32"),
+    "li": ("sbuf", [128, 416], "bfloat16"), "tb": ("sbuf", [128, 416], "bfloat16"), "nu": ("sbuf", [128, 416], "bfloat16"),
+    "tt": ("sbuf", [128, 800], "bfloat16"), "tq": ("sbuf", [128, 800], "bfloat16"), "tn": ("sbuf", [128, 800], "bfloat16"),
+    "td": ("sbuf", [128, 192], "float32"), "dd": ("sbuf", [128, 192], "float32"), "dz": ("sbuf", [128, 192], "float32"),
+    "nn": ("sbuf", [128, 384], "bfloat16"),
+    "zn": ("sbuf", [128, 1536], "bfloat16"), "nmu": ("sbuf", [128, 384], "float32"),
     "bw": ("sbuf", [128, 384], "bfloat16"), "eu": ("sbuf", [128, 224], "bfloat16"), "ew": ("sbuf", [128, 64], "uint16"),
-    "dn": ("sbuf", [128, 1536], "bfloat16"), "vo": ("sbuf", [128, 768], "bfloat16"), "vf": ("sbuf", [128, 768], "bfloat16"),
-    "qvo": ("sbuf", [128, 192], "float8_e4m3fn_x4"), "svo": ("sbuf", [128, 192], "uint8"),
-    "qvf": ("sbuf", [128, 192], "float8_e4m3fn_x4"), "svf": ("sbuf", [128, 192], "uint8"),
+    "dn": ("sbuf", [128, 1536], "bfloat16"), "vv": ("sbuf", [128, 1536], "bfloat16"),
+    "qv": ("sbuf", [128, 384], "float8_e4m3fn_x4"), "sv": ("sbuf", [128, 384], "uint8"),
     "ysb": ("sbuf", [128, 384], "float32"),
     "pa": ("psum", [128, 2048], "float32"), "pb": ("psum", [128, 2048], "float32"),
 }
 for _r in range(ROUNDS):
     SCRATCH["nw%d" % _r] = ("sbuf", [128, 32], "uint16")
-    SCRATCH["ns%d" % _r] = ("sbuf", [128, 32], "uint16")
-    SCRATCH["st%d" % _r] = ("sbuf", [128, 64], "uint16")
+    SCRATCH["ns%d" % _r] = ("sbuf", [128, 24], "uint16")
     SCRATCH["fin%d" % _r] = ("sbuf", [128, 48], "uint16")
     SCRATCH["ip%d" % _r] = ("sbuf", [128, 24], "uint16")
     SCRATCH["qz%d" % _r] = ("sbuf", [128, 384], "float8_e4m3fn_x4")
@@ -47,14 +44,17 @@ for _r in range(ROUNDS):
     SCRATCH["lz%d" % _r] = ("sbuf", [128, 384], "uint8")
 for _r in range(3):
     SCRATCH["ow%d" % _r] = ("sbuf", [128, 32], "uint16")
-    SCRATCH["nx%d" % _r] = ("sbuf", [128, 32], "uint16")
+    SCRATCH["nx%d" % _r] = ("sbuf", [128, 24], "uint16")
+    SCRATCH["sw%d" % _r] = ("sbuf", [128, 32], "uint16")
+    SCRATCH["no%d" % _r] = ("sbuf", [128, 32], "uint16")
 
-SEMAPHORES = ["cV", "cS", "cP", "cG", "sent"] + ["d%d" % k for k in range(24)] \
-    + ["al%d" % k for k in range(ROUNDS)] + ["az%d" % k for k in range(2 * ROUNDS)]
+SEMAPHORES = ["cV", "cS", "cP", "cG", "sent"] + ["d%d" % k for k in range(48)] \
+    + ["al%d" % k for k in range(ROUNDS)] + ["az%d" % k for k in range(3 * ROUNDS)]
 
-AFTER = ("z0", "z1", "n", "nwrap", "bw", "eu", "unpack0:VVSS", "ewrap", "vo:SVSV", "unpack1:SVSS", "own", "vf:VSSS",
-         "renew_own:VSSS", "far", "ahead", "codes_own", "renew_far:SSSV", "score_own:S", "codes_far", "diffs", "nmove",
-         "score_far:V", "names")
+AFTER = """z:0:0123 z:1:0 leave:0 z:1:123 z:2:0 leave:1 z:2:123 leave:2 tn:0 tn:1 nw bw back eu
+unpack:0 dn:0:0V1S2S3S te:0 te:1 unpack:1 dn:1:0S1S ew:012 v:o:0S dn:1:2S ew:3 v:o:1S2V3V dn:1:3V
+unpack:2 dn:2:0S1V layer:o dn:2:2S3S v:f:0V1V2S3S add:o:0 layer:f add:o:123 x:o:0S1S2S3S
+add:f:0123 x:f:0S1S2V3S codes:o codes:f names score:o:V score:f:V""".split()
 
 
 def rank_program(g, core, T, topo):
@@ -105,7 +105,7 @@ def rank_program(g, core, T, topo):
                     lst[:] = [e for e in lst if not (n[1] <= e[1] and e[2] <= n[2])]
                 lst.append((tok, n[1], n[2], n[3], w))
 
-    def op(q, fn, reads=(), writes=(), dma=False):
+    def op(q, fn, reads=(), writes=(), dmas=()):
         toks = []
         for w, ks in ((False, reads), (True, writes)):
             for k in ks:
@@ -114,11 +114,12 @@ def rank_program(g, core, T, topo):
                     if (w or e[4]) and meets(e, n):
                         toks.append(e[0])
         wait(q, toks)
-        if dma:
-            s, v = "d%d" % ndma[0], 16
+        if dmas:
+            s, v = "d%d" % ndma[0], 16 * len(dmas)
             ndma[0] += 1
             total[s] = v
-            fn(queue[q]).then_inc(T.sem[s], 16)
+            for out, src in dmas:
+                queue[q].dma_start(out, src).then_inc(T.sem[s], 16)
         else:
             s = "c" + q
             total[s] = v = total.get(s, 0) + 1
@@ -143,9 +144,9 @@ def rank_program(g, core, T, topo):
                                       T[rq][:, ra:ra + n], T[rs][:, ra:ra + n], True, True),
            [(lq, la, la + 128), (ls, la, la + 128), (rq, ra, ra + n)], [key])
 
-    def quant(q, s, src, a, n, t=0):
-        op("V", lambda e: e.quantize_mx(T[q][:, a:a + n], T[s][:, a:a + n], T[src][:, t:t + 4 * n]),
-           [(src, t, t + 4 * n)], [(q, a, a + n)])
+    def quant(q, s, src, a, n):
+        op("V", lambda e: e.quantize_mx(T[q][:, a:a + n], T[s][:, a:a + n], T[src][:, 4 * a:4 * a + 4 * n]),
+           [(src, 4 * a, 4 * a + 4 * n)], [(q, a, a + n)])
 
     def ts(out, i, s1, s2, o0, o1, reads, writes):
         if o1 is None:
@@ -171,8 +172,13 @@ def rank_program(g, core, T, topo):
         else:
             act(out, a, reads, writes)
 
-    def load(q, out, src, key):
-        op(q, lambda e: e.dma_start(out, src), [], [key], dma=True)
+    def dma(q, out, src, reads, writes):
+        op(q, None, reads, writes, [(out, src)])
+
+    def shift(dst, src, a, n, by, step=1):
+        p = 16 * (by % 8)
+        op("Y", None, [(src, a, a + n)], [(dst, 0, n)],
+           [(T[dst][p:128:step, 0:n], T[src][0:128 - p:step, a:a + n]), (T[dst][0:p:step, 0:n], T[src][128 - p:128:step, a:a + n])])
 
     def iota(out, pattern, base, keys, cm=0, whole=False):
         if whole:
@@ -180,17 +186,15 @@ def rank_program(g, core, T, topo):
         else:
             op("G", lambda e: e.iota(out, pattern, base, cm, allow_small_or_imprecise_dtypes=True), [], keys)
 
-    def fill(out, keys):
-        op("V", lambda e: e.memset(out, 0.0), [], keys)
-
-    moved = ["mv%d" % a for a in range(4)]
-    load("Y", T.nlb[48:128, :], T.nl[0:80, :], "nlb.a")
-    load("S", T.nlb[0:48, :], T.nl[80:128, :], "nlb.b")
-    load("Y", T.ua[:, :], T.u[:, :], ("ua", 0, 512))
-    load("S", T.xt[:, :], T.x[:, :], ("xt", 0, 1536))
-    load("Y", T.wq[:, :].bitcast(dt.uint8), T.wc[:, :], ("wq", 0, 512))
-    load("Y", T.wp[:, :], T.ws[:, :], ("wp", 0, 512))
-    load("Y", T.vt[:, :], T.v[:, :], ("vt", 0, 512))
+    dma("Y", T.nlb[48:128, 0:24], T.nl[0:80, :], [], ["nlb.a"])
+    dma("S", T.nlb[0:48, 0:24], T.nl[80:128, :], [], ["nlb.b"])
+    dma("Y", T.nlb[32:128, 24:48], T.nl[0:96, :], [], ["nlb.c"])
+    dma("S", T.nlb[0:32, 24:48], T.nl[96:128, :], [], ["nlb.d"])
+    dma("Y", T.ua[:, :], T.u[:, :], [], ["ua"])
+    dma("S", T.xt[:, :], T.x[:, :], [], ["xt"])
+    dma("Y", T.wq[:, :].bitcast(dt.uint8), T.wc[:, :], [], ["wq"])
+    dma("Y", T.wp[:, :], T.ws[:, :], [], ["wp"])
+    dma("Y", T.vt[:, :], T.v[:, :], [], ["vt"])
 
     def kc(i, n=3):
         return T.kk[:, 8 * i:8 * i + n]
@@ -204,283 +208,274 @@ def rank_program(g, core, T, topo):
     iota(kc(1), [[16, 3]], 0, kr(1), 0, True)
     iota(kc(2, 8), [[16, 8]], 80, kr(2), 0, True)
     iota(T.ci[:, :], [[1, 384]], -192, ["ci"])
-    iota(T.tt[:, MV:2 * MV], [[0, MV]], 0, moved)
-    iota(T.te[:, :], [[0, 800]], 0, ["te"])
     iota(T.one[:, :], [[0, 512]], 1, ["one"])
     for b in range(4):
         op("G", lambda e: e.affine_select(T.et[:, 512 * b:512 * b + 512], T.one[:, :], [[1, 512]], A.is_equal, 0.0, -b, -4),
            ["one"], [("et", 512 * b, 512 * b + 512)])
-    iota(T.nmt[:, :], [[1, 2], [2, 192]], 0, ["nmt"])
-    fill(T.td[:, :], ["td"])
-    for buf, end in (("li", 400), ("nu", 400), ("eu", 208)):
-        fill(T[buf][:, 0:16], [(buf, 0, 16)])
-        fill(T[buf][:, end:end + 16], [(buf, end, end + 16)])
+    act(T.td[:, :], T.ci[:, 0:192], ["ci"], ["td"])
+    for buf, end in (("li", 400), ("tb", 400), ("nu", 400), ("eu", 208)):
+        act(T[buf][:, 0:16], T.ci[:, 0:16], ["ci"], [(buf, 0, 16)])
+        act(T[buf][:, end:end + 16], T.ci[:, 0:16], ["ci"], [(buf, end, end + 16)])
 
-    def const(c, n, add, by=None):
-        if by is None:
-            ts(T.clu[:, c:c + n], kc(10, n), add, None, A.add, None, kr(10), [("clu", c, c + n)])
-        else:
-            ts(T.clu[:, c:c + n], kc(10, n), col(by), add, A.add, A.add, kr(10) + [("kf", by, by + 1)], [("clu", c, c + n)])
+    OWN = (0, 2, 4)
+
+    def const(row, n):
+        ts(T.clu[:, OWN[row]:OWN[row] + n], kc(10, n), float(row), None, A.add, None, kr(10), [("clu", OWN[row], OWN[row] + n)])
     ts(kc(3, 1), kc(0, 1), 15, None, A.bitwise_and, None, kr(0), kr(3))
     ts(kc(4, 1), kc(0, 1), 4, None, A.logical_shift_right, None, kr(0), kr(4))
     cp(col(0), kc(3, 1), kr(3), [("kf", 0, 1)])
     tt(kc(5, 1), kc(0, 1), kc(4, 1), A.add, kr(0, 4), kr(5))
-    ts(kc(6, 1), kc(4, 1), 1, None, A.bitwise_and, None, kr(4), kr(6))
+    ts(col(1), kc(3, 1), 17.0, None, A.mult, None, kr(3), [("kf", 1, 2)])
     ts(kc(7), kc(1), col(0), None, A.add, None, kr(1) + [("kf", 0, 1)], kr(7))
     ts(kc(5, 1), kc(5, 1), 1, None, A.bitwise_and, None, kr(5), kr(5))
-    ts(col(1), kc(3, 1), 17.0, None, A.mult, None, kr(3), [("kf", 1, 2)])
+    ts(kc(11, 8), kc(2, 8), col(1), None, A.add, None, kr(2) + [("kf", 1, 2)], kr(11))
     ts(kc(8), kc(7), 24.0, -24.0, A.is_ge, A.mult, kr(7), kr(8))
     ts(col(2), kc(5, 1), 400.0, None, A.mult, None, kr(5), [("kf", 2, 3)])
-    ts(kc(11, 8), kc(2, 8), col(1), None, A.add, None, kr(2) + [("kf", 1, 2)], kr(11))
-    tt(kc(9), kc(7), kc(8), A.add, kr(7, 8), kr(9))
-    ts(col(3), kc(6, 1), 768.0, 16.0, A.mult, A.add, kr(6), [("kf", 3, 4)])
     ts(kc(11, 8), kc(11, 8), 127, None, A.bitwise_and, None, kr(11), kr(11))
-    ts(kc(10), kc(9), 16.0, col(2), A.mult, A.add, kr(9) + [("kf", 2, 3)], kr(10))
-    ts(col(4), kc(6, 1), -17.0, 3.0, A.mult, A.add, kr(6), [("kf", 4, 5)])
+    tt(kc(9), kc(7), kc(8), A.add, kr(7, 8), kr(9))
     cp(T.ul[:, :], kc(11, 8), kr(11), ["ul"])
-    OWN, NEXT, SRC, NSRC = (0, 4, 10), (2, 6), 8, 14
-    const(OWN[0], 2, 0.0)
-    const(NEXT[0], 2, 0.0, 3)
+    ts(kc(10), kc(9), 16.0, col(2), A.mult, A.add, kr(9) + [("kf", 2, 3)], kr(10))
+    const(0, 2)
+    const(1, 2)
+    const(2, 3)
 
-    nl = ["nlb.a", "nlb.b"]
-    ts(T.nla[:, 0:24], T.nlb[:, :], 1, None, A.bitwise_and, None, nl, [("nla", 0, 24)])
-    ts(T.nla[:, 24:48], T.nlb[:, :], 1, None, A.logical_shift_right, None, nl, [("nla", 24, 48)])
-    ts(T.nla[:, 48:72], T.nla[:, 0:24], 192, None, A.mult, None, [("nla", 0, 24)], [("nla", 48, 72)])
-    const(OWN[1], 2, 1.0)
-    tt(T.nla[:, 72:96], T.nla[:, 24:48], T.nla[:, 48:72], A.add, [("nla", 24, 72)], [("nla", 72, 96)])
-    const(NEXT[1], 2, 1.0, 3)
-    cp(T.pn[:, :], T.nla[:, 72:96], [("nla", 72, 96)], ["pn"])
+    nl = ["nlb.a", "nlb.b", "nlb.c", "nlb.d"]
+    ts(T.nla[:, 0:48], T.nlb[:, :], 1, None, A.bitwise_and, None, nl, [("nla", 0, 48)])
+    ts(T.nla[:, 48:96], T.nlb[:, :], 1, None, A.logical_shift_right, None, nl, [("nla", 48, 96)])
+    ts(T.nla[:, 96:144], T.nla[:, 0:48], 192, None, A.mult, None, [("nla", 0, 48)], [("nla", 96, 144)])
+    tt(T.nla[:, 144:192], T.nla[:, 48:96], T.nla[:, 96:144], A.add, [("nla", 48, 144)], [("nla", 144, 192)])
+    cp(T.pn[:, :], T.nla[:, 144:192], [("nla", 144, 192)], ["pn"])
     quant("qua", "sua", "ua", 0, 128)
-    cp(T.li[:, 16:400].indirect(T.pn[:, :]), T.ci[:, :], ["pn", "ci"], [("li", 16, 400)])
-    cp(T.qub[:, :].bitcast(dt.uint32), T.qua[:, :].bitcast(dt.uint32).indirect(T.ul[:, :]), ["qua", "ul"], ["qub"])
+    cp(T.li[:, 16:400].indirect(T.pn[:, 0:24]), T.ci[:, :], ["pn", "ci"], [("li", 16, 400)])
     act(T.sub[:, :], T.sua[:, :].indirect(T.ul[:, :]), ["qua", "ul"], ["sub"])
-    quant("qx", "sx", "xt", 0, 384)
-    mm(0, 384, "qub", "sub", 0, "qx", "sx", 0)
+    act(T.nn[:, :], T.ci[:, :].indirect(T.pn[:, 24:48]), ["ci", "pn"], ["nn"])
+    cp(T.qub[:, :].bitcast(dt.uint32), T.qua[:, :].bitcast(dt.uint32).indirect(T.ul[:, :]), ["qua", "ul"], ["qub"])
 
-    def transposes(dst, src, n=384):
-        op("V", lambda e: e.transpose(T[dst][:, 0:n], T[src][:, 16:16 + n]), [(src, 16, 16 + n)], [(dst, 0, n)])
-        op("V", lambda e: e.transpose(T[dst][:, 384:416 + n], T[src][:, 0:n + 32]), [(src, 0, n + 32)], [(dst, 384, 416 + n)])
+    def transpose(k, dst, src, n=384):
+        if k == 0:
+            op("V", lambda e: e.transpose(T[dst][:, 0:n], T[src][:, 16:16 + n]), [(src, 16, 16 + n)], [(dst, 0, n)])
+        else:
+            op("V", lambda e: e.transpose(T[dst][:, 384:416 + n], T[src][:, 0:n + 32]), [(src, 0, n + 32)], [(dst, 384, 416 + n)])
 
-    def move(src, row, step, to, by):
-        n = 64 if by == 2 else 32
-        for a in range(0, 128, n):
-            b = (a + 32 * by) % 128
-            act(T.tt[b:b + n, MV + to:2 * MV:step], T[src][a:a + n, row:MV:step], [(src, 0, MV)],
-                [("mv%d" % k, to, MV, step) for k in range(b // 32, (b + n) // 32)])
+    def table(out, src, row, n=2):
+        ts(T[out][:, 0:16 * n], T[src][:, :].indirect(T.clu[:, OWN[row]:OWN[row] + n]), 192.0, None, A.add, None,
+           [("clu", OWN[row], OWN[row] + n), src], [out])
 
-    def table(out, src, a, b, c, n, extra=()):
-        ts(T[out][:, 0:16 * n], T[src][:, a:b].indirect(T.clu[:, c:c + n]), 192.0, None, A.add, None,
-           [("clu", c, c + n)] + ([(src, 0, MV)] if a == 0 else []) + (moved if b > MV else []), [out])
-
-    def diff(to, step, a, b, reads):
-        tt(T.td[:, to:192:step], T.tt[:, a + 192:a + 384:step], T.tt[:, a:a + 192:step], A.subtract, reads, [("td", to, 192, step)])
-
-    def diff_back():
-        op("V", lambda e: e.transpose(T.dd[:, :], T.td[:, :]), [("td", 0, 192)], ["dd"])
-
-    def wrap(k, row, to):
-        transposes("tt", "li")
-        move("tt", row, 32, row, 3)
+    def diff(row, to):
         tt(T.td[:, to:192:16], T.tt[:, row + 192:384:16], T.tt[:, row:192:16], A.subtract, [("tt", 0, 384)], [("td", to, 192, 16)])
-        table("ow%d" % k, "tt", 0, MV, OWN[row], 2)
-        diff_back()
 
-    def unwrap(lst, a):
-        act(T.lin[:, :], T.ci[:, :].indirect(T[lst][:, a:a + 24]), ["ci", lst], ["lin"])
+    def diff_back(out):
+        op("V", lambda e: e.transpose(T[out][:, :], T.td[:, :]), ["td"], [out])
 
     def send(dst, out, src, sem):
         rid, pid = topo.addr(dst, core)
         g.remote_dma(out, src, T.sem[sem], T.sem.sent, pid, rid, topo.mask(core, dst))
         total["sent"] = total.get("sent", 0) + len(topo.engines(core, dst))
 
-    wrap(0, 0, 0)
-    ts(T.fl[:, :], T.pa[:, 0:384], 0.0, None, A.is_gt, None, ["bank0"], [("fl", 0, 384), "bank0"])
-    table("nx0", "tt", 0, 2 * MV, NEXT[0], 2)
-    unwrap("nx0", 0)
+    def flags(j, a, q):
+        buf, c, key = bank(j)
+        if q == "V":
+            ts(T.fl[:, a:a + 192], buf[:, c:c + 192], 0.0, None, A.is_gt, None, [key], [("fl", a, a + 192), key])
+        else:
+            op("S", lambda e: e.activation(T.sg[:, :], buf[:, c:c + 192], Sign), [key], ["sg", key])
+            op("S", lambda e: e.activation(T.fl[:, a:a + 192], T.sg[:, :], Relu), ["sg"], [("fl", a, a + 192)])
+
+    quant("qx", "sx", "xt", 0, 384)
+    mm(0, 192, "qub", "sub", 0, "qx", "sx", 192)
+    mm(1, 192, "qub", "sub", 0, "qx", "sx", 0)
+    flags(0, 192, "S")
+    transpose(0, "tt", "li")
+    transpose(1, "tt", "li")
+    diff(0, 0)
+    table("ow0", "tt", 0)
+    shift("nx0", "ow0", 0, 24, -1)
+    diff_back("dd")
+    flags(1, 0, "V")
     for r in range(ROUNDS):
         last = r == ROUNDS - 1
         to, frm = T.cores[(rank + STEPS[r]) % N], T.cores[(rank - STEPS[r]) % N]
         nin = len(topo.engines(frm, core))
-        nw, qz, sz, lq, lz, ip, fin, st, ns = ("%s%d" % (k, r) for k in ("nw", "qz", "sz", "lq", "lz", "ip", "fin", "st", "ns"))
+        nw, qz, sz, lq, lz, ip, fin, ns = ("%s%d" % (k, r) for k in ("nw", "qz", "sz", "lq", "lz", "ip", "fin", "ns"))
 
-        def beside(j):
-            for t in ((0,), (1, 2), (3,))[j]:
-                act(T.xh[:, 384 * t:384 * t + 384], T.xt[:, t:1536:4], [("xt", t, 1536, 4)],
-                    [("xh", 384 * t, 384 * t + 384)], scale=0.5)
-            for t in ((0,), (1,), (2, 3))[j]:
-                for h in range(2):
-                    o = 384 * t + 192 * h
-                    act(T.xg[:, o:o + 192], T.xt[:, 4 * h + t:1536:8], [("xt", 4 * h + t, 1536, 8)],
-                        [("xg", o, o + 192)], scale=0.5)
-            if j == 1 and r == 0:
-                act(T.yb[:, :], T.xt[:, :], [("xt", 0, 1536)], [("yb", 0, 1536)], scale=32.0)
+        def halves(t):
+            act(T.xh[:, 384 * t:384 * t + 384], T.xt[:, t:1536:4], [("xt", t, 1536, 4)], [("xh", 384 * t, 384 * t + 384)], scale=0.5)
+            for h in range(2):
+                o = 384 * t + 192 * h
+                op("G", lambda e: e.affine_select(T.xg[:, o:o + 192], T.xh[:, 384 * t + h:384 * t + 384:2], [[0, 192]],
+                                                  A.is_ge, 0.0, 0, 0), [("xh", 384 * t, 384 * t + 384)], [("xg", o, o + 192)])
+
+        def constants(k):
+            if r == 0 and k < 4:
+                quant("qe", "se", "et", 128 * k, 128)
+            if r == 1 and k == 0:
+                quant("qvt", "svt", "vt", 0, 128)
+        if r == 1:
+            iota(T.nmt[:, :], [[1, 2], [2, 192]], 0, ["nmt"])
         for j in range(3):
-            if j == 0 and r > 0:
-                iw, nx, na, own = "st%d" % (r - 1), "st%d" % (r - 1), 32, "ns%d" % (r - 1)
-            else:
-                iw, nx, na, own = "ow%d" % j, "nx%d" % j, 0, "pn"
+            iw, nx, sw = "ow%d" % j, "nx%d" % j, "sw%d" % j
+            own = "no%d" % j if j else "ns%d" % (r - 1) if r else "pn"
+            if j:
+                transpose(0, "tn", "nu")
             tt(T.pp[:, 0:192], T.fl[:, 0:384].indirect(T[iw][:, 0:12]), T.dd[:, :], A.mult, ["fl", iw, "dd"], [("pp", 0, 192)])
             if j == 0:
-                if r == 0:
-                    const(SRC, 2, 0.0, 4)
+                halves(0)
                 ts(T.pp[:, 192:384], T.pp[:, 0:192], -1.0, None, A.mult, None, [("pp", 0, 192)], [("pp", 192, 384)])
-                if r == 0:
-                    const(OWN[2], 3, 2.0)
-                act(T.dl[:, 192:384], T.pp[:, 0:384].indirect(T[own][:, 12:24]), [("pp", 0, 384), own], [("dl", 192, 384)])
-                cp(T.dl[:, 0:192], T.pp[:, 0:384].indirect(T[own][:, 0:12]), [("pp", 0, 384), own], [("dl", 0, 192)])
-                if r == 0:
-                    const(NSRC, 2, 2.0, 4)
             else:
-                table(nx, "tt", 0, 2 * MV, NEXT[j - 1], 2)
                 act(T.pp[:, 192:384], T.pp[:, 0:192], [("pp", 0, 192)], [("pp", 192, 384)], scale=-1.0)
-                unwrap(nx, 0)
-                for h in range(2):
-                    cp(T.dl[:, 0:384].indirect(T[iw][:, 12 * h:12 * h + 12]), T.pp[:, 192 * h:192 * h + 192],
-                       [("pp", 192 * h, 192 * h + 192), iw], ["dl"])
-            tt(T.li[:, 16:400], T.dl[:, 0:384].indirect(T[nx][:, na:na + 24]), T.lin[:, :], A.add,
-               ["dl", nx, "lin"], [("li", 16, 400)])
-            beside(j)
+                transpose(1, "tn", "nu")
+                table(own, "tn", 0)
+            tt(T.tb[:, 16:400], T.pp[:, 0:384].indirect(T[own][:, 0:24]), T.ci[:, :], A.add,
+               [("pp", 0, 384), own, "ci"], [("tb", 16, 400)])
             if j < 2:
-                wrap(j + 1, j, j + 1)
-        transposes("tt", "li")
-        table(fin, "tt", 0, MV, OWN[2], 3)
+                halves(2 * j + 1)
+            act(T.li[:, 16:400], T.tb[:, 16:400].indirect(T[nx][:, 0:24]), [("tb", 16, 400), nx], [("li", 16, 400)])
+            if j:
+                constants(2 * j - 1)
+            transpose(0, "tq", "tb")
+            transpose(1, "tq", "tb")
+            table(sw, "tq", j)
+            act(T.nu[:, 16:400], T.nn[:, :].indirect(T[sw][:, 0:24]), ["nn", sw], [("nu", 16, 400)])
+            if j < 2:
+                constants(2 * j)
+            transpose(0, "tt", "li")
+            transpose(1, "tt", "li")
+            if j < 2:
+                diff(j, j + 1)
+                table("ow%d" % (j + 1), "tt", j)
+                shift("nx%d" % (j + 1), "ow%d" % (j + 1), 0, 24, -1)
+                diff_back("dd")
+                shift("nn", "nu", 16, 384, -1, 16)
+            if j == 0:
+                halves(2)
+        if not last:
+            diff(2, 0)
+        table(fin, "tt", 2, 3)
         wait("G", [("cV", total["cV"])])
         send(to, T[ip][:, 0:24], T[fin][:, 0:24], "al%d" % r)
         note(("al%d" % r, nin), [], [ip])
         total["al%d" % r] = nin
         if not last:
-            move("tt", 2, 16, 2, 1)
-            move("tt", 18, 32, 3, 2)
+            shift("ow0", fin, 0, 12, 3)
+            shift("nx0", fin, 0, 24, 2)
+            shift("nn", "nu", 16, 384, 2, 16)
+        if r == 0:
+            act(T.yb[:, :], T.xt[:, :], ["xt"], ["yb"], scale=32.0)
 
-        def z(h, _):
-            a, b = PARTS[h]
-            az = "az%d" % (2 * r + h)
-            for t in range(4):
+        half = {"f": 0, "o": 192}
+
+        def pairs(s):
+            return [(int(a), b) for a, b in zip(s[::2], s[1::2])]
+
+        def z(h, which):
+            a, b = PARTS[int(h)]
+            for t in map(int, which):
                 tt(T.zn[:, 4 * a + t:4 * b:4], T.xh[:, 384 * t:384 * t + 384].indirect(T[fin][:, 12 + a // 16:12 + b // 16]),
                    T.xg[:, 384 * t + a:384 * t + b], A.add, [("xh", 384 * t, 384 * t + 384), ("xg", 384 * t, 384 * t + 384), fin],
                    [("zn", 4 * a + t, 4 * b, 4)])
-            quant(qz, sz, "zn", a, b - a, 4 * a)
+
+        def leave(h):
+            a, b = PARTS[int(h)]
+            az = "az%d" % (3 * r + int(h))
+            quant(qz, sz, "zn", a, b - a)
             wait("G", [("cV", total["cV"])])
             send(to, T[lq][:, a:b].bitcast(dt.uint8), T[qz][:, a:b].bitcast(dt.uint8), az)
             send(to, T[lz][:, a:b], T[sz][:, a:b], az)
             total[az] = 2 * nin
             note((az, 2 * nin), [], [(lq, a, b)])
 
-        def names_by_column(_):
-            cp(T.nu[:, 16:400].indirect(T[fin][:, 0:24]), T.ci[:, :], [fin, "ci"], [("nu", 16, 400)])
-            if r == 0:
-                quant("qe", "se", "et", 0, 512)
+        def names_table():
+            table(nw, "tn", 0)
+            if not last:
+                shift(ns, nw, 0, 24, 3)
 
-        def nwrap(_):
-            transposes("tn", "nu")
-            table(nw, "tn", 0, MV, OWN[0], 2)
-
-        def bw(_):
+        def bw():
             act(T.bw[:, :], T.nu[:, 16:400].indirect(T[ip][:, 0:24]), [("nu", 16, 400), ip], ["bw"])
 
-        def eu(_):
+        def eu():
             act(T.eu[:, 16:208], T.bw[:, 0:384].indirect(T[nw][:, 12:24]), ["bw", nw], [("eu", 16, 208)])
 
-        def ewrap(_):
-            transposes("te", "eu", 192)
-            for t in range(4):
-                ts(T.ew[:, 16 * t:16 * t + 16], T.te[:, 0:800].indirect(T.clu[:, 0:1]), 4.0, 768.0 + t, A.mult, A.add,
-                   ["te", ("clu", 0, 2)], [("ew", 16 * t, 16 * t + 16)])
+        def ew(which):
+            for t in map(int, which):
+                ts(T.ew[:, 16 * t:16 * t + 16], T.tq[:, :].indirect(T.clu[:, 0:1]), 4.0, 768.0 + t, A.mult, A.add,
+                   ["tq", ("clu", 0, 2)], [("ew", 16 * t, 16 * t + 16)])
 
-        def vo(qs):
-            for t in range(4):
-                copy_on(qs[t], T.vo[:, t:768:4], T.zn[:, 0:1536].indirect(T.ew[:, 16 * t:16 * t + 12]),
-                        [("zn", 0, 1536), ("ew", 16 * t, 16 * t + 16)], [("vo", t, 768, 4)])
-
-        def unpack(h, qs):
-            p, e = PARTS[h]
-            js = take(4)
+        def unpack(h):
+            p, e = PARTS[int(h)]
+            held[h] = take(4)
             for b in range(4):
-                mm(js[b], e - p, "qe", "se", 128 * b, lq, lz, p)
-            for b in range(4):
-                buf, c, key = bank(js[b])
-                o = 384 * b
-                copy_on(qs[b], T.dn[:, o + p:o + e], buf[:, c:c + e - p], [key], [key, ("dn", o + p, o + e)])
-            spare.extend(js)
+                mm(held[h][b], e - p, "qe", "se", 128 * b, lq, lz, p)
 
-        def vf(qs):
-            for t in range(4):
-                copy_on(qs[t], T.vf[:, t:768:4], T.dn[:, 384 * t:384 * t + 384].indirect(T[nw][:, 0:12]),
-                        [("dn", 384 * t, 384 * t + 384), nw], [("vf", t, 768, 4)])
+        def dn(h, which):
+            p, e = PARTS[int(h)]
+            for b, q in pairs(which):
+                buf, c, key = bank(held[h][b])
+                copy_on(q, T.dn[:, 384 * b + p:384 * b + e], buf[:, c:c + e - p], [key], [key, ("dn", 384 * b + p, 384 * b + e)])
+                spare.append(held[h][b])
 
-        def layer(o, q, s, v):
-            quant(q, s, v, 0, 192)
-            held[o] = take(4)
-            for b in range(4):
-                mm(held[o][b], 192, "wq", "wp", 128 * b, q, s, 0)
+        def v(h, which):
+            o = 4 * half[h]
+            for t, q in pairs(which):
+                if h == "f":
+                    src, reads = T.dn[:, 384 * t:384 * t + 384].indirect(T[nw][:, 0:12]), [("dn", 384 * t, 384 * t + 384), nw]
+                else:
+                    src, reads = T.zn[:, :].indirect(T.ew[:, 16 * t:16 * t + 12]), ["zn", ("ew", 16 * t, 16 * t + 16)]
+                copy_on(q, T.vv[:, o + t:o + 768:4], src, reads, [("vv", o + t, o + 768, 4)])
 
-        def renew(o, qs):
+        def layer(h):
+            quant("qv", "sv", "vv", half[h], 192)
+            held[h] = take(4)
             for b in range(4):
-                buf, c, key = bank(held[o][b])
+                mm(held[h][b], 192, "wq", "wp", 128 * b, "qv", "sv", half[h])
+
+        def add(h, which):
+            o = 4 * half[h]
+            for b in map(int, which):
+                buf, c, key = bank(held[h][b])
                 y = T.yb[:, o + b:o + 768:4]
                 tt(y, buf[:, c:c + 192], y, A.add, [key, ("yb", o + b, o + 768, 4)], [key, ("yb", o + b, o + 768, 4)])
+                spare.append(held[h][b])
+
+        def x(h, which):
+            o = 4 * half[h]
+            for b, q in pairs(which):
                 k = ([("yb", o + b, o + 768, 4)], [("xt", o + b, o + 768, 4)])
-                if qs[b] == "S":
-                    act(T.xt[:, o + b:o + 768:4], y, *k, scale=2.0 ** -5)
+                if q == "S":
+                    act(T.xt[:, o + b:o + 768:4], T.yb[:, o + b:o + 768:4], *k, scale=2.0 ** -5)
                 else:
-                    ts(T.xt[:, o + b:o + 768:4], y, 2.0 ** -5, None, A.mult, None, *k)
-            spare.extend(held[o])
+                    ts(T.xt[:, o + b:o + 768:4], T.yb[:, o + b:o + 768:4], 2.0 ** -5, None, A.mult, None, *k)
 
-        def codes(o):
-            quant("qx", "sx", "xt", o // 4, 192, o)
+        def codes(h):
+            a = half[h]
+            quant("qx", "sx", "xt", a, 192)
             if last:
-                op("Y", lambda e: e.dma_start(T.oc[:, o:o + 768], T.qx[:, o // 4:o // 4 + 192].bitcast(dt.uint8)),
-                   [("qx", o // 4, o // 4 + 192)], [], dma=True)
+                dma("Y", T.oc[:, 4 * a:4 * a + 768], T.qx[:, a:a + 192].bitcast(dt.uint8), [("qx", a, a + 192)], [])
 
-        def score(a, q):
-            j = take(1)[0]
+        def score(h, q):
+            a, j = half[h], take(1)[0]
             buf, c, key = bank(j)
             if last:
                 mm(j, 192, "qvt", "svt", 0, "qx", "sx", a)
                 copy_on(q, T.ysb[:, a:a + 192], buf[:, c:c + 192], [key], [("ysb", a, a + 192), key])
-                op("S", lambda e: e.dma_start(T.y[:, a:a + 192], T.ysb[:, a:a + 192]), [("ysb", a, a + 192)], [], dma=True)
+                dma("S", T.y[:, a:a + 192], T.ysb[:, a:a + 192], [("ysb", a, a + 192)], [])
             else:
                 mm(j, 192, "qub", "sub", 0, "qx", "sx", a)
-                if q == "V":
-                    ts(T.fl[:, a:a + 192], buf[:, c:c + 192], 0.0, None, A.is_gt, None, [key], [("fl", a, a + 192), key])
-                else:
-                    op("S", lambda e: e.activation(T.sg[:, :], buf[:, c:c + 192], Sign), [key], ["sg", key])
-                    op("S", lambda e: e.activation(T.fl[:, a:a + 192], T.sg[:, :], Relu), ["sg"], [("fl", a, a + 192)])
+                flags(j, a, q)
             spare.append(j)
 
-        def ahead(_):
-            if r == 0:
-                quant("qvt", "svt", "vt", 0, 128)
+        def back():
             if not last:
-                table(st, "tt", MV, 2 * MV, SRC, 4)
-                unwrap(st, 32)
+                diff_back("dz")
+                shift("dd", "dz", 0, 192, 3, 16)
 
-        def diffs(_):
-            if not last:
-                diff(0, 32, MV + 3, 0, moved)
-                diff(16, 32, MV + 2, 0, moved)
-                diff_back()
-
-        def nmove(_):
+        def names():
             if last:
                 act(T.nmu[:, :], T.nmt[:, :].indirect(T[nw][:, 0:24]), ["nmt", nw], ["nmu"])
-                op("Y", lambda e: e.dma_start(T.nm[:, :], T.nmu[0:128:16, :]), ["nmu"], [], dma=True)
-            else:
-                move("tn", 0, 32, 4, 1)
-                move("tn", 16, 32, 5, 2)
+                dma("Y", T.nm[:, :], T.nmu[0:128:16, :], ["nmu"], [])
 
-        def names(_):
-            if not last:
-                table(ns, "tt", MV, 2 * MV, NSRC, 2)
-
-        steps = {"z0": lambda q: z(0, q), "z1": lambda q: z(1, q), "n": names_by_column, "nwrap": nwrap, "bw": bw, "eu": eu,
-                 "ewrap": ewrap, "vo": vo, "vf": vf, "unpack0": lambda q: unpack(0, q), "unpack1": lambda q: unpack(1, q),
-                 "far": lambda q: layer(0, "qvf", "svf", "vf"), "own": lambda q: layer(768, "qvo", "svo", "vo"),
-                 "renew_far": lambda q: renew(0, q), "renew_own": lambda q: renew(768, q),
-                 "codes_far": lambda q: codes(0), "codes_own": lambda q: codes(768), "nmove": nmove, "diffs": diffs,
-                 "score_far": lambda q: score(0, q), "score_own": lambda q: score(192, q), "ahead": ahead, "names": names}
+        steps = {"z": z, "leave": leave, "tn": lambda k: transpose(int(k), "tn", "nu"), "nw": names_table, "bw": bw, "eu": eu,
+                 "te": lambda k: transpose(int(k), "tq", "eu", 192), "ew": ew, "unpack": unpack, "dn": dn, "v": v, "layer": layer,
+                 "add": add, "x": x, "codes": codes, "score": score, "back": back, "names": names}
         for s in AFTER:
-            steps[s.split(":")[0]](s.split(":")[-1])
-    for k in range(4):
-        op("YSYS"[k], lambda e: e.dma_start(T.osc[4 * k:4 * k + 4, :], T.sx[32 * k:32 * k + 4, 0:384]), [("qx", 0, 384)], [], dma=True)
+            steps[s.split(":")[0]](*s.split(":")[1:])
+    op("Y", None, ["qx"], [], [(T.osc[4 * k:4 * k + 4, :], T.sx[32 * k:32 * k + 4, 0:384]) for k in range(4)])
     wait("G", sorted(total.items()))

from concourse.bass import DstId, RemoteDMATransfer
from concourse.mybir import dt, AluOpType, ActivationFunctionType

C, H, N = 384, 192, 8
ROUNDS = 3
STEPS = [4, 1, 2]
PARTS = ((0, 128), (128, 256), (256, 384))

SCRATCH = {
    "xt": ("sbuf", [128, 1536], "bfloat16"), "yb": ("sbuf", [128, 1536], "bfloat16"),
    "xh": ("sbuf", [128, 1536], "bfloat16"), "xg": ("sbuf", [128, 1536], "bfloat16"),
    "qx": ("sbuf", [128, 384], "float8_e4m3fn_x4"), "sx": ("sbuf", [128, 384], "uint8"),
    "ua": ("sbuf", [128, 512], "bfloat16"), "vt": ("sbuf", [128, 512], "bfloat16"),
    "qua": ("sbuf", [128, 128], "float8_e4m3fn_x4"), "sua": ("sbuf", [128, 128], "uint8"),
    "qub": ("sbuf", [128, 128], "float8_e4m3fn_x4"), "sub": ("sbuf", [128, 128], "uint8"),
    "qvt": ("sbuf", [128, 128], "float8_e4m3fn_x4"), "svt": ("sbuf", [128, 128], "uint8"),
    "wq": ("sbuf", [128, 512], "float8_e4m3fn_x4"), "wp": ("sbuf", [128, 512], "uint8"),
    "nlb": ("sbuf", [128, 48], "int32"), "nla": ("sbuf", [128, 192], "int32"), "pn": ("sbuf", [128, 48], "uint16"),
    "kk": ("sbuf", [128, 96], "int32"), "kf": ("sbuf", [128, 8], "float32"), "clu": ("sbuf", [128, 8], "uint16"),
    "ul": ("sbuf", [128, 8], "uint16"),
    "ci": ("sbuf", [128, 384], "bfloat16"), "nmt": ("sbuf", [128, 384], "float32"),
    "one": ("sbuf", [128, 512], "bfloat16"), "et": ("sbuf", [128, 2048], "bfloat16"),
    "qe": ("sbuf", [128, 512], "float8_e4m3fn_x4"), "se": ("sbuf", [128, 512], "uint8"),
    "sg": ("sbuf", [128, 192], "bfloat16"), "fl": ("sbuf", [128, 384], "bfloat16"), "pp": ("sbuf", [128, 384], "float32"),
    "li": ("sbuf", [128, 416], "bfloat16"), "tb": ("sbuf", [128, 416], "bfloat16"), "nu": ("sbuf", [128, 416], "bfloat16"),
    "tt": ("sbuf", [128, 800], "bfloat16"), "tq": ("sbuf", [128, 800], "bfloat16"), "tn": ("sbuf", [128, 800], "bfloat16"),
    "td": ("sbuf", [128, 192], "float32"), "dd": ("sbuf", [128, 192], "float32"), "dz": ("sbuf", [128, 192], "float32"),
    "nn": ("sbuf", [128, 384], "bfloat16"),
    "zn": ("sbuf", [128, 1536], "bfloat16"), "nmu": ("sbuf", [128, 384], "float32"),
    "bw": ("sbuf", [128, 384], "bfloat16"), "eu": ("sbuf", [128, 224], "bfloat16"), "ew": ("sbuf", [128, 64], "uint16"),
    "dn": ("sbuf", [128, 1536], "bfloat16"), "vv": ("sbuf", [128, 1536], "bfloat16"),
    "qv": ("sbuf", [128, 384], "float8_e4m3fn_x4"), "sv": ("sbuf", [128, 384], "uint8"),
    "ysb": ("sbuf", [128, 384], "float32"),
    "pa": ("psum", [128, 2048], "float32"), "pb": ("psum", [128, 2048], "float32"),
}
for _r in range(ROUNDS):
    SCRATCH["nw%d" % _r] = ("sbuf", [128, 32], "uint16")
    SCRATCH["ns%d" % _r] = ("sbuf", [128, 24], "uint16")
    SCRATCH["fin%d" % _r] = ("sbuf", [128, 48], "uint16")
    SCRATCH["ip%d" % _r] = ("sbuf", [128, 24], "uint16")
    SCRATCH["qz%d" % _r] = ("sbuf", [128, 384], "float8_e4m3fn_x4")
    SCRATCH["sz%d" % _r] = ("sbuf", [128, 384], "uint8")
    SCRATCH["lq%d" % _r] = ("sbuf", [128, 384], "float8_e4m3fn_x4")
    SCRATCH["lz%d" % _r] = ("sbuf", [128, 384], "uint8")
for _r in range(3):
    SCRATCH["ow%d" % _r] = ("sbuf", [128, 32], "uint16")
    SCRATCH["nx%d" % _r] = ("sbuf", [128, 24], "uint16")
    SCRATCH["sw%d" % _r] = ("sbuf", [128, 32], "uint16")
    SCRATCH["no%d" % _r] = ("sbuf", [128, 32], "uint16")

SEMAPHORES = ["cV", "cS", "cP", "cG", "sent"] + ["d%d" % k for k in range(48)] \
    + ["al%d" % k for k in range(ROUNDS)] + ["az%d" % k for k in range(3 * ROUNDS)]

AFTER = """z:0:0123 z:1:0 leave:0 z:1:123 z:2:0 leave:1 z:2:123 leave:2 tn:0 tn:1 nw bw back eu
unpack:0 dn:0:0V1S2S3S te:0 te:1 unpack:1 dn:1:0S1S ew:012 v:o:0S dn:1:2S ew:3 v:o:1S2V3V dn:1:3V
unpack:2 dn:2:0S1V layer:o dn:2:2S3S v:f:0V1V2S3S add:o:0 layer:f add:o:123 x:o:0S1S2S3S
add:f:0123 x:f:0S1S2V3S codes:o codes:f names score:o:V score:f:V""".split()


def rank_program(g, core, T, topo):
    rank = T.rank_of(core)
    if rank is None:
        return
    A = AluOpType
    Copy, Sign, Relu = ActivationFunctionType.Copy, ActivationFunctionType.Sign, ActivationFunctionType.Relu

    queue = {"V": g.vector, "S": g.scalar, "P": g.tensor, "G": g, "Y": g.sync}
    known = {q: {} for q in queue}
    done = {}
    total = {}
    acc = {}
    ndma = [0]

    def gcd(a, b):
        while b:
            a, b = b, a % b
        return a

    def meets(a, b):
        if a[2] <= b[1] or b[2] <= a[1]:
            return False
        return (a[1] - b[1]) % gcd(a[3], b[3]) == 0

    def norm(k):
        return (k, 0, 1 << 20, 1) if isinstance(k, str) else tuple(k) + (1,) * (4 - len(k))

    def wait(q, toks):
        best = {}
        for s, v in toks:
            if known[q].get(s, 0) < v:
                best[s] = max(best.get(s, 0), v)
        need = list(best.items())
        keep = [t for t in need if not any(o != t and done.get(o, {}).get(t[0], 0) >= t[1] for o in need)]
        for s, v in keep:
            queue[q].wait_ge(T.sem[s], v)
            for a, b in list(done.get((s, v), {}).items()) + [(s, v)]:
                known[q][a] = max(known[q].get(a, 0), b)

    def note(tok, reads, writes):
        for w, ks in ((False, reads), (True, writes)):
            for k in ks:
                n = norm(k)
                lst = acc.setdefault(n[0], [])
                if w and n[3] == 1:
                    lst[:] = [e for e in lst if not (n[1] <= e[1] and e[2] <= n[2])]
                lst.append((tok, n[1], n[2], n[3], w))

    def op(q, fn, reads=(), writes=(), dmas=()):
        toks = []
        for w, ks in ((False, reads), (True, writes)):
            for k in ks:
                n = norm(k)
                for e in acc.get(n[0], ()):
                    if (w or e[4]) and meets(e, n):
                        toks.append(e[0])
        wait(q, toks)
        if dmas:
            s, v = "d%d" % ndma[0], 16 * len(dmas)
            ndma[0] += 1
            total[s] = v
            for out, src in dmas:
                queue[q].dma_start(out, src).then_inc(T.sem[s], 16)
        else:
            s = "c" + q
            total[s] = v = total.get(s, 0) + 1
            fn(queue[q]).then_inc(T.sem[s], 1)
        done[(s, v)] = dict(known[q])
        note((s, v), reads, writes)

    def bank(j):
        return (T.pa if j < 4 else T.pb), 512 * (j % 4), "bank%d" % j

    spare, held = list(range(8)), {}

    def take(n):
        js = spare[:n]
        del spare[:n]
        assert len(js) == n
        return js

    def mm(j, n, lq, ls, la, rq, rs, ra):
        buf, o, key = bank(j)
        op("P", lambda e: e.matmul_mx(buf[:, o:o + n], T[lq][:, la:la + 128], T[ls][:, la:la + 128],
                                      T[rq][:, ra:ra + n], T[rs][:, ra:ra + n], True, True),
           [(lq, la, la + 128), (ls, la, la + 128), (rq, ra, ra + n)], [key])

    def quant(q, s, src, a, n):
        op("V", lambda e: e.quantize_mx(T[q][:, a:a + n], T[s][:, a:a + n], T[src][:, 4 * a:4 * a + 4 * n]),
           [(src, 4 * a, 4 * a + 4 * n)], [(q, a, a + n)])

    def ts(out, i, s1, s2, o0, o1, reads, writes):
        if o1 is None:
            op("V", lambda e: e.tensor_scalar(out, i, s1, None, o0), reads, writes)
        else:
            op("V", lambda e: e.tensor_scalar(out, i, s1, s2, o0, o1), reads, writes)

    def tt(out, a, b, o, reads, writes):
        op("V", lambda e: e.tensor_tensor(out, a, b, o), reads, writes)

    def cp(out, a, reads, writes):
        op("V", lambda e: e.tensor_copy(out, a), reads, writes)

    def act(out, a, reads, writes, scale=1.0):
        if scale == 1.0:
            op("S", lambda e: e.activation(out, a, Copy), reads, writes)
        else:
            op("S", lambda e: e.activation(out, a, Copy, scale=scale), reads, writes)

    def copy_on(q, out, a, reads, writes):
        if q == "V":
            cp(out, a, reads, writes)
        else:
            act(out, a, reads, writes)

    def dma(q, out, src, reads, writes):
        op(q, None, reads, writes, [(out, src)])

    def shift(dst, src, a, n, by, step=1):
        p = 16 * (by % 8)
        op("Y", None, [(src, a, a + n)], [(dst, 0, n)],
           [(T[dst][p:128:step, 0:n], T[src][0:128 - p:step, a:a + n]), (T[dst][0:p:step, 0:n], T[src][128 - p:128:step, a:a + n])])

    def iota(out, pattern, base, keys, cm=0, whole=False):
        if whole:
            op("G", lambda e: e.iota(out, pattern, base, cm), [], keys)
        else:
            op("G", lambda e: e.iota(out, pattern, base, cm, allow_small_or_imprecise_dtypes=True), [], keys)

    dma("Y", T.nlb[48:128, 0:24], T.nl[0:80, :], [], ["nlb.a"])
    dma("S", T.nlb[0:48, 0:24], T.nl[80:128, :], [], ["nlb.b"])
    dma("Y", T.nlb[32:128, 24:48], T.nl[0:96, :], [], ["nlb.c"])
    dma("S", T.nlb[0:32, 24:48], T.nl[96:128, :], [], ["nlb.d"])
    dma("Y", T.ua[:, :], T.u[:, :], [], ["ua"])
    dma("S", T.xt[:, :], T.x[:, :], [], ["xt"])
    dma("Y", T.wq[:, :].bitcast(dt.uint8), T.wc[:, :], [], ["wq"])
    dma("Y", T.wp[:, :], T.ws[:, :], [], ["wp"])
    dma("Y", T.vt[:, :], T.v[:, :], [], ["vt"])

    def kc(i, n=3):
        return T.kk[:, 8 * i:8 * i + n]

    def kr(*i):
        return [("kk", 8 * j, 8 * j + 8) for j in i]

    def col(i):
        return T.kf[:, i:i + 1]
    iota(kc(0, 1), [[0, 1]], 0, kr(0), 1, True)
    iota(kc(1), [[16, 3]], 0, kr(1), 0, True)
    iota(kc(2, 8), [[16, 8]], 80, kr(2), 0, True)
    iota(T.ci[:, :], [[1, 384]], -192, ["ci"])
    iota(T.one[:, :], [[0, 512]], 1, ["one"])
    for b in range(4):
        op("G", lambda e: e.affine_select(T.et[:, 512 * b:512 * b + 512], T.one[:, :], [[1, 512]], A.is_equal, 0.0, -b, -4),
           ["one"], [("et", 512 * b, 512 * b + 512)])
    act(T.td[:, :], T.ci[:, 0:192], ["ci"], ["td"])
    for buf, end in (("li", 400), ("tb", 400), ("nu", 400), ("eu", 208)):
        act(T[buf][:, 0:16], T.ci[:, 0:16], ["ci"], [(buf, 0, 16)])
        act(T[buf][:, end:end + 16], T.ci[:, 0:16], ["ci"], [(buf, end, end + 16)])

    OWN = (0, 2, 4)

    def const(row, n):
        ts(T.clu[:, OWN[row]:OWN[row] + n], kc(10, n), float(row), None, A.add, None, kr(10), [("clu", OWN[row], OWN[row] + n)])
    ts(kc(3, 1), kc(0, 1), 15, None, A.bitwise_and, None, kr(0), kr(3))
    ts(kc(4, 1), kc(0, 1), 4, None, A.logical_shift_right, None, kr(0), kr(4))
    cp(col(0), kc(3, 1), kr(3), [("kf", 0, 1)])
    tt(kc(5, 1), kc(0, 1), kc(4, 1), A.add, kr(0, 4), kr(5))
    ts(col(1), kc(3, 1), 17.0, None, A.mult, None, kr(3), [("kf", 1, 2)])
    ts(kc(7), kc(1), col(0), None, A.add, None, kr(1) + [("kf", 0, 1)], kr(7))
    ts(kc(5, 1), kc(5, 1), 1, None, A.bitwise_and, None, kr(5), kr(5))
    ts(kc(11, 8), kc(2, 8), col(1), None, A.add, None, kr(2) + [("kf", 1, 2)], kr(11))
    ts(kc(8), kc(7), 24.0, -24.0, A.is_ge, A.mult, kr(7), kr(8))
    ts(col(2), kc(5, 1), 400.0, None, A.mult, None, kr(5), [("kf", 2, 3)])
    ts(kc(11, 8), kc(11, 8), 127, None, A.bitwise_and, None, kr(11), kr(11))
    tt(kc(9), kc(7), kc(8), A.add, kr(7, 8), kr(9))
    cp(T.ul[:, :], kc(11, 8), kr(11), ["ul"])
    ts(kc(10), kc(9), 16.0, col(2), A.mult, A.add, kr(9) + [("kf", 2, 3)], kr(10))
    const(0, 2)
    const(1, 2)
    const(2, 3)

    nl = ["nlb.a", "nlb.b", "nlb.c", "nlb.d"]
    ts(T.nla[:, 0:48], T.nlb[:, :], 1, None, A.bitwise_and, None, nl, [("nla", 0, 48)])
    ts(T.nla[:, 48:96], T.nlb[:, :], 1, None, A.logical_shift_right, None, nl, [("nla", 48, 96)])
    ts(T.nla[:, 96:144], T.nla[:, 0:48], 192, None, A.mult, None, [("nla", 0, 48)], [("nla", 96, 144)])
    tt(T.nla[:, 144:192], T.nla[:, 48:96], T.nla[:, 96:144], A.add, [("nla", 48, 144)], [("nla", 144, 192)])
    cp(T.pn[:, :], T.nla[:, 144:192], [("nla", 144, 192)], ["pn"])
    quant("qua", "sua", "ua", 0, 128)
    cp(T.li[:, 16:400].indirect(T.pn[:, 0:24]), T.ci[:, :], ["pn", "ci"], [("li", 16, 400)])
    act(T.sub[:, :], T.sua[:, :].indirect(T.ul[:, :]), ["qua", "ul"], ["sub"])
    act(T.nn[:, :], T.ci[:, :].indirect(T.pn[:, 24:48]), ["ci", "pn"], ["nn"])
    cp(T.qub[:, :].bitcast(dt.uint32), T.qua[:, :].bitcast(dt.uint32).indirect(T.ul[:, :]), ["qua", "ul"], ["qub"])

    def transpose(k, dst, src, n=384):
        if k == 0:
            op("V", lambda e: e.transpose(T[dst][:, 0:n], T[src][:, 16:16 + n]), [(src, 16, 16 + n)], [(dst, 0, n)])
        else:
            op("V", lambda e: e.transpose(T[dst][:, 384:416 + n], T[src][:, 0:n + 32]), [(src, 0, n + 32)], [(dst, 384, 416 + n)])

    def table(out, src, row, n=2):
        ts(T[out][:, 0:16 * n], T[src][:, :].indirect(T.clu[:, OWN[row]:OWN[row] + n]), 192.0, None, A.add, None,
           [("clu", OWN[row], OWN[row] + n), src], [out])

    def diff(row, to):
        tt(T.td[:, to:192:16], T.tt[:, row + 192:384:16], T.tt[:, row:192:16], A.subtract, [("tt", 0, 384)], [("td", to, 192, 16)])

    def diff_back(out):
        op("V", lambda e: e.transpose(T[out][:, :], T.td[:, :]), ["td"], [out])

    def send(dst, out, src, sem):
        rid, pid = topo.addr(dst, core)
        g.remote_dma(out, src, T.sem[sem], T.sem.sent, pid, rid, topo.mask(core, dst))
        total["sent"] = total.get("sent", 0) + len(topo.engines(core, dst))

    def flags(j, a, q):
        buf, c, key = bank(j)
        if q == "V":
            ts(T.fl[:, a:a + 192], buf[:, c:c + 192], 0.0, None, A.is_gt, None, [key], [("fl", a, a + 192), key])
        else:
            op("S", lambda e: e.activation(T.sg[:, :], buf[:, c:c + 192], Sign), [key], ["sg", key])
            op("S", lambda e: e.activation(T.fl[:, a:a + 192], T.sg[:, :], Relu), ["sg"], [("fl", a, a + 192)])

    quant("qx", "sx", "xt", 0, 384)
    mm(0, 192, "qub", "sub", 0, "qx", "sx", 192)
    mm(1, 192, "qub", "sub", 0, "qx", "sx", 0)
    flags(0, 192, "S")
    transpose(0, "tt", "li")
    transpose(1, "tt", "li")
    diff(0, 0)
    table("ow0", "tt", 0)
    shift("nx0", "ow0", 0, 24, -1)
    diff_back("dd")
    flags(1, 0, "V")
    for r in range(ROUNDS):
        last = r == ROUNDS - 1
        to, frm = T.cores[(rank + STEPS[r]) % N], T.cores[(rank - STEPS[r]) % N]
        nin = len(topo.engines(frm, core))
        nw, qz, sz, lq, lz, ip, fin, ns = ("%s%d" % (k, r) for k in ("nw", "qz", "sz", "lq", "lz", "ip", "fin", "ns"))

        def halves(t):
            act(T.xh[:, 384 * t:384 * t + 384], T.xt[:, t:1536:4], [("xt", t, 1536, 4)], [("xh", 384 * t, 384 * t + 384)], scale=0.5)
            for h in range(2):
                o = 384 * t + 192 * h
                op("G", lambda e: e.affine_select(T.xg[:, o:o + 192], T.xh[:, 384 * t + h:384 * t + 384:2], [[0, 192]],
                                                  A.is_ge, 0.0, 0, 0), [("xh", 384 * t, 384 * t + 384)], [("xg", o, o + 192)])

        def constants(k):
            if r == 0 and k < 4:
                quant("qe", "se", "et", 128 * k, 128)
            if r == 1 and k == 0:
                quant("qvt", "svt", "vt", 0, 128)
        if r == 1:
            iota(T.nmt[:, :], [[1, 2], [2, 192]], 0, ["nmt"])
        for j in range(3):
            iw, nx, sw = "ow%d" % j, "nx%d" % j, "sw%d" % j
            own = "no%d" % j if j else "ns%d" % (r - 1) if r else "pn"
            if j:
                transpose(0, "tn", "nu")
            tt(T.pp[:, 0:192], T.fl[:, 0:384].indirect(T[iw][:, 0:12]), T.dd[:, :], A.mult, ["fl", iw, "dd"], [("pp", 0, 192)])
            if j == 0:
                halves(0)
                ts(T.pp[:, 192:384], T.pp[:, 0:192], -1.0, None, A.mult, None, [("pp", 0, 192)], [("pp", 192, 384)])
            else:
                act(T.pp[:, 192:384], T.pp[:, 0:192], [("pp", 0, 192)], [("pp", 192, 384)], scale=-1.0)
                transpose(1, "tn", "nu")
                table(own, "tn", 0)
            tt(T.tb[:, 16:400], T.pp[:, 0:384].indirect(T[own][:, 0:24]), T.ci[:, :], A.add,
               [("pp", 0, 384), own, "ci"], [("tb", 16, 400)])
            if j < 2:
                halves(2 * j + 1)
            act(T.li[:, 16:400], T.tb[:, 16:400].indirect(T[nx][:, 0:24]), [("tb", 16, 400), nx], [("li", 16, 400)])
            if j:
                constants(2 * j - 1)
            transpose(0, "tq", "tb")
            transpose(1, "tq", "tb")
            table(sw, "tq", j)
            act(T.nu[:, 16:400], T.nn[:, :].indirect(T[sw][:, 0:24]), ["nn", sw], [("nu", 16, 400)])
            if j < 2:
                constants(2 * j)
            transpose(0, "tt", "li")
            transpose(1, "tt", "li")
            if j < 2:
                diff(j, j + 1)
                table("ow%d" % (j + 1), "tt", j)
                shift("nx%d" % (j + 1), "ow%d" % (j + 1), 0, 24, -1)
                diff_back("dd")
                shift("nn", "nu", 16, 384, -1, 16)
            if j == 0:
                halves(2)
        if not last:
            diff(2, 0)
        table(fin, "tt", 2, 3)
        wait("G", [("cV", total["cV"])])
        send(to, T[ip][:, 0:24], T[fin][:, 0:24], "al%d" % r)
        note(("al%d" % r, nin), [], [ip])
        total["al%d" % r] = nin
        if not last:
            shift("ow0", fin, 0, 12, 3)
            shift("nx0", fin, 0, 24, 2)
            shift("nn", "nu", 16, 384, 2, 16)
        if r == 0:
            act(T.yb[:, :], T.xt[:, :], ["xt"], ["yb"], scale=32.0)

        half = {"f": 0, "o": 192}

        def pairs(s):
            return [(int(a), b) for a, b in zip(s[::2], s[1::2])]

        def z(h, which):
            a, b = PARTS[int(h)]
            for t in map(int, which):
                tt(T.zn[:, 4 * a + t:4 * b:4], T.xh[:, 384 * t:384 * t + 384].indirect(T[fin][:, 12 + a // 16:12 + b // 16]),
                   T.xg[:, 384 * t + a:384 * t + b], A.add, [("xh", 384 * t, 384 * t + 384), ("xg", 384 * t, 384 * t + 384), fin],
                   [("zn", 4 * a + t, 4 * b, 4)])

        def leave(h):
            a, b = PARTS[int(h)]
            az = "az%d" % (3 * r + int(h))
            quant(qz, sz, "zn", a, b - a)
            wait("G", [("cV", total["cV"])])
            send(to, T[lq][:, a:b].bitcast(dt.uint8), T[qz][:, a:b].bitcast(dt.uint8), az)
            send(to, T[lz][:, a:b], T[sz][:, a:b], az)
            total[az] = 2 * nin
            note((az, 2 * nin), [], [(lq, a, b)])

        def names_table():
            table(nw, "tn", 0)
            if not last:
                shift(ns, nw, 0, 24, 3)

        def bw():
            act(T.bw[:, :], T.nu[:, 16:400].indirect(T[ip][:, 0:24]), [("nu", 16, 400), ip], ["bw"])

        def eu():
            act(T.eu[:, 16:208], T.bw[:, 0:384].indirect(T[nw][:, 12:24]), ["bw", nw], [("eu", 16, 208)])

        def ew(which):
            for t in map(int, which):
                ts(T.ew[:, 16 * t:16 * t + 16], T.tq[:, :].indirect(T.clu[:, 0:1]), 4.0, 768.0 + t, A.mult, A.add,
                   ["tq", ("clu", 0, 2)], [("ew", 16 * t, 16 * t + 16)])

        def unpack(h):
            p, e = PARTS[int(h)]
            held[h] = take(4)
            for b in range(4):
                mm(held[h][b], e - p, "qe", "se", 128 * b, lq, lz, p)

        def dn(h, which):
            p, e = PARTS[int(h)]
            for b, q in pairs(which):
                buf, c, key = bank(held[h][b])
                copy_on(q, T.dn[:, 384 * b + p:384 * b + e], buf[:, c:c + e - p], [key], [key, ("dn", 384 * b + p, 384 * b + e)])
                spare.append(held[h][b])

        def v(h, which):
            o = 4 * half[h]
            for t, q in pairs(which):
                if h == "f":
                    src, reads = T.dn[:, 384 * t:384 * t + 384].indirect(T[nw][:, 0:12]), [("dn", 384 * t, 384 * t + 384), nw]
                else:
                    src, reads = T.zn[:, :].indirect(T.ew[:, 16 * t:16 * t + 12]), ["zn", ("ew", 16 * t, 16 * t + 16)]
                copy_on(q, T.vv[:, o + t:o + 768:4], src, reads, [("vv", o + t, o + 768, 4)])

        def layer(h):
            quant("qv", "sv", "vv", half[h], 192)
            held[h] = take(4)
            for b in range(4):
                mm(held[h][b], 192, "wq", "wp", 128 * b, "qv", "sv", half[h])

        def add(h, which):
            o = 4 * half[h]
            for b in map(int, which):
                buf, c, key = bank(held[h][b])
                y = T.yb[:, o + b:o + 768:4]
                tt(y, buf[:, c:c + 192], y, A.add, [key, ("yb", o + b, o + 768, 4)], [key, ("yb", o + b, o + 768, 4)])
                spare.append(held[h][b])

        def x(h, which):
            o = 4 * half[h]
            for b, q in pairs(which):
                k = ([("yb", o + b, o + 768, 4)], [("xt", o + b, o + 768, 4)])
                if q == "S":
                    act(T.xt[:, o + b:o + 768:4], T.yb[:, o + b:o + 768:4], *k, scale=2.0 ** -5)
                else:
                    ts(T.xt[:, o + b:o + 768:4], T.yb[:, o + b:o + 768:4], 2.0 ** -5, None, A.mult, None, *k)

        def codes(h):
            a = half[h]
            quant("qx", "sx", "xt", a, 192)
            if last:
                dma("Y", T.oc[:, 4 * a:4 * a + 768], T.qx[:, a:a + 192].bitcast(dt.uint8), [("qx", a, a + 192)], [])

        def score(h, q):
            a, j = half[h], take(1)[0]
            buf, c, key = bank(j)
            if last:
                mm(j, 192, "qvt", "svt", 0, "qx", "sx", a)
                copy_on(q, T.ysb[:, a:a + 192], buf[:, c:c + 192], [key], [("ysb", a, a + 192), key])
                dma("S", T.y[:, a:a + 192], T.ysb[:, a:a + 192], [("ysb", a, a + 192)], [])
            else:
                mm(j, 192, "qub", "sub", 0, "qx", "sx", a)
                flags(j, a, q)
            spare.append(j)

        def back():
            if not last:
                diff_back("dz")
                shift("dd", "dz", 0, 192, 3, 16)

        def names():
            if last:
                act(T.nmu[:, :], T.nmt[:, :].indirect(T[nw][:, 0:24]), ["nmt", nw], ["nmu"])
                dma("Y", T.nm[:, :], T.nmu[0:128:16, :], ["nmu"], [])

        steps = {"z": z, "leave": leave, "tn": lambda k: transpose(int(k), "tn", "nu"), "nw": names_table, "bw": bw, "eu": eu,
                 "te": lambda k: transpose(int(k), "tq", "eu", 192), "ew": ew, "unpack": unpack, "dn": dn, "v": v, "layer": layer,
                 "add": add, "x": x, "codes": codes, "score": score, "back": back, "names": names}
        for s in AFTER:
            steps[s.split(":")[0]](*s.split(":")[1:])
    op("Y", None, ["qx"], [], [(T.osc[4 * k:4 * k + 4, :], T.sx[32 * k:32 * k + 4, 0:384]) for k in range(4)])
    wait("G", sorted(total.items()))
